import numpy as np
import ml_dtypes


def mxq(x, axis, fmt="e4m3"):
    dtype, down = {"e4m3": (ml_dtypes.float8_e4m3fn, 7), "e5m2": (ml_dtypes.float8_e5m2, 14)}[fmt]
    v = np.moveaxis(np.asarray(x, np.float32).astype(ml_dtypes.bfloat16).astype(np.float64), axis, -1)
    blocks = v.reshape(v.shape[:-1] + (-1, 32))
    amax = np.abs(blocks).max(-1, keepdims=True)
    byte = np.maximum(np.where(amax > 0, np.frexp(amax)[1] - 1 + 127, 0) - down, 1)
    scale = np.exp2(byte - 127.0)
    codes = (blocks / scale).astype(np.float32).astype(dtype).astype(np.float64)
    return np.moveaxis((codes * scale).reshape(v.shape), -1, axis)


WIDE = False


def mx_kscale(k):
    if not WIDE:
        return np.ones(k)
    levels = np.array([10, -10, 5, -5, 0])
    if k % 512:
        return np.exp2(np.random.permutation(np.resize(levels, k // 32))).repeat(32)
    a = np.empty((k // 512, 16))
    for p in range(k // 512):
        a[p, :8] = np.random.permutation(np.resize(levels, 8))
        for g in range(8):
            far = levels[np.abs(levels - a[p, g]) >= 10]
            a[p, g + 8] = far[np.random.randint(len(far))]
    return np.exp2(a.ravel()).repeat(32)


def f64(x):
    return np.asarray(x).astype(np.float64)


def striped(idx):
    return np.tile(idx.reshape(-1, 16).T, (8, 1)).astype(np.uint16)


def unstriped(offs):
    return offs[:16].T.reshape(-1).astype(np.int64)


def pack_weight(w):
    k, n = w.shape
    w = f64(np.asarray(w, np.float32).astype(ml_dtypes.bfloat16)).reshape(k // 32, 32, n)
    amax = np.abs(w).max(1)
    byte = np.clip(np.where(amax > 0, np.frexp(amax)[1] - 1 + 127 - 7, 1), 1, 254)
    scaled = (w * np.exp2(127.0 - byte)[:, None, :]).reshape(k, n).astype(np.float32)
    words = np.ascontiguousarray(scaled.reshape(k // 512, 128, 4, n).transpose(0, 1, 3, 2)).astype(ml_dtypes.float8_e4m3fn).view(np.uint8)
    return words, np.ascontiguousarray(byte.astype(np.uint8).reshape(k // 512, 16, n))


def unpack_weight(words, scales):
    g, p, n, _ = words.shape
    vals = np.ascontiguousarray(words).view(ml_dtypes.float8_e4m3fn).astype(np.float64) * np.repeat(np.exp2(scales.astype(np.float64) - 127.0), 8, axis=1)[..., None]
    return vals.transpose(0, 1, 3, 2).reshape(g * 512, n)


def planes(y):
    n, m = y.shape
    v = y.astype(np.float32).astype(ml_dtypes.bfloat16).astype(np.float64).reshape(n // 32, 32, m)
    top = np.abs(v).max(1)
    byte = np.clip(np.where(top > 0, np.frexp(top)[1] - 1 + 127 - 7, 1), 1, 254)
    codes = (v * np.exp2(127.0 - byte)[:, None, :]).reshape(n, m).astype(np.float32).astype(ml_dtypes.float8_e4m3fn).view(np.uint8)
    words = codes.reshape(n // 512, 128, 4, m).transpose(0, 1, 3, 2)
    return np.ascontiguousarray(words), np.ascontiguousarray(byte.astype(np.uint8).reshape(n // 512, 16, m))


def relu(v):
    return np.maximum(v, 0.0)


K, T, S, H, N, V = 512, 1024, 512, 512, 512, 128


def setup_inputs():
    n = np.random.standard_normal
    s = mx_kscale(K)[:, None]
    u = mx_kscale(H)
    near = np.random.permutation(S)
    packed_xT = pack_weight(n((K, T)) * s)
    return {
        "x_words": packed_xT[0],
        "x_scales": packed_xT[1],
        "w1": (n((K, H)) / np.sqrt(K) / s * u).astype(np.float32),
        "w2": (n((H, N)) / np.sqrt(H) / u[:, None]).astype(np.float32),
        "offs": striped(np.random.permutation(T)[:S]),
        "give": striped(near[:V]),
        "take": striped(near[V : 2 * V]),
    }


def reference(x_words, x_scales, w1, w2, offs, give, take):
    xq = unpack_weight(x_words, x_scales)[:, unstriped(offs)]
    h = relu(mxq(f64(w1), 0, "e4m3").T @ xq)
    z = h.copy()
    z[:, unstriped(take)] = h[:, unstriped(give)]
    out_0 = mxq(f64(w2), 0, "e4m3").T @ mxq(z, 0, "e4m3")
    return (out_0,) + planes(out_0)

@@ -1,0 +1,225 @@
+from contextlib import ExitStack
+
+import concourse.mybir as mybir
+
+F32 = mybir.dt.float32
+BF16 = mybir.dt.bfloat16
+I32 = mybir.dt.int32
+U32 = mybir.dt.uint32
+U16 = mybir.dt.uint16
+U8 = mybir.dt.uint8
+FP8X4 = mybir.dt.float8_e4m3fn_x4
+RELU = mybir.ActivationFunctionType.Relu
+COPY = mybir.ActivationFunctionType.Copy
+
+P = 128
+PACK = 4
+T = 1024
+S = 512
+H = 512
+N = 512
+V = 128
+CHUNK = 128
+HALF = 256
+LAST = 3
+FLOPS = 2 * 2 * 512 * 512 * 512
+
+
+def tile_picked_ycutmix_relu_po_kernel(
+    tc, x_words, x_scales, w1, w2, offs, give, take, out_0, out_1, out_2
+):
+    nc = tc.nc
+    with ExitStack() as ctx:
+        lists = ctx.enter_context(tc.tile_pool(name="lists", bufs=1))
+        keep = ctx.enter_context(tc.tile_pool(name="keep", bufs=1))
+        psum = ctx.enter_context(tc.psum_pool(name="psum", bufs=1))
+
+        offs_t = lists.tile([P, S // 16], U16, name="offs_t")
+        give_t = lists.tile([P, V // 16], U16, name="give_t")
+        take_t = lists.tile([P, V // 16], U16, name="take_t")
+
+        xw = keep.tile([P, T], I32, name="xw", align_bytes=64)
+        xs = keep.tile([P, T], U8, name="xs", align_bytes=64)
+        w1_raw = keep.tile([P, PACK, H], F32, name="w1_raw", align_bytes=64)
+        w2_raw = keep.tile([P, PACK, N], F32, name="w2_raw", tag="w2_then_planes", align_bytes=64)
+
+        nc.vector.memset(xs[:].bitcast(I32), 0)
+        warm = keep.tile([P, 2], F32, name="warm")
+        nc.gpsimd.memset(warm[:, 0:1], 0.0)
+        nc.scalar.activation(warm[:, 1:2], warm[:, 0:1], RELU)
+        nc.sync.dma_start(offs_t[:], offs)
+        nc.sync.dma_start(give_t[:], give)
+        nc.sync.dma_start(xw[:], x_words[0].rearrange("p n t -> p (n t)").bitcast(I32))
+        for q in range(4):
+            nc.sync.dma_start(xs[32 * q : 32 * q + 4, :].bitcast(I32), x_scales[0, 4 * q : 4 * q + 4, :].bitcast(I32))
+        w1_rows = w1.rearrange("(p j) c -> p j c", j=PACK)
+        nc.sync.dma_start(w1_raw[:, 0:2], w1_rows[:, 0:2])
+        nc.sync.dma_start(w1_raw[:, 2:4], w1_rows[:, 2:4])
+        nc.sync.dma_start(take_t[:], take)
+        w2_rows = w2.rearrange("(b s r) n -> s b r n", s=PACK, r=8)
+        for s in range(PACK):
+            nc.sync.dma_start(w2_raw[:, s, :], w2_rows[s])
+
+        xq_w = keep.tile([P, S], U32, name="xq_w", align_bytes=64)
+        xq_s = keep.tile([P, S], U8, name="xq_s", align_bytes=64)
+        nc.vector.tensor_copy(xq_w[:], xw[:].bitcast(U32).indirect(offs_t[:]))
+        nc.vector.tensor_copy(xq_s[:], xs[:].indirect(offs_t[:]))
+
+        w1_view = w1_raw[:].rearrange("p j (b s r) -> p s b j r", s=PACK, r=8)
+        w1_g = [keep.tile([P, P * PACK], BF16, name=f"w1_g{s}", align_bytes=64) for s in range(PACK)]
+        w1_c = [keep.tile([P, P], U32, name=f"w1_c{s}", align_bytes=64) for s in range(PACK)]
+        w1_s = [keep.tile([P, P], U8, name=f"w1_s{s}", align_bytes=64) for s in range(PACK)]
+        banks = [psum.tile([P, 512], F32, name=f"bank{b}") for b in range(8)]
+        z = [keep.tile([P, S], F32, name=f"z{s}", align_bytes=64) for s in range(PACK)]
+        picked = [keep.tile([P, V], F32, name=f"picked{s}", align_bytes=64) for s in range(PACK)]
+
+        def cast_w1(s, blocks, on_vector):
+            dst = w1_g[s][:].rearrange("p (b r j) -> p b j r", r=8, j=PACK)[:, blocks]
+            if on_vector:
+                nc.vector.tensor_copy(dst, w1_view[:, s, blocks])
+            else:
+                nc.scalar.activation(dst, w1_view[:, s, blocks], COPY)
+
+        def quant_w1(s):
+            nc.vector.quantize_mx(out=w1_c[s][:].bitcast(FP8X4), scales=w1_s[s][:], in_=w1_g[s][:])
+
+        def layer1(s, half):
+            cols = slice(half * HALF, (half + 1) * HALF)
+            nc.tensor.matmul_mx(
+                out=banks[2 * s + half][:, 0:HALF], lhsT=w1_c[s][:].bitcast(FP8X4), lhsT_scale=w1_s[s][:],
+                rhs=xq_w[:, cols].bitcast(FP8X4), rhs_scale=xq_s[:, cols], start=True, stop=True,
+            )
+
+        def relu_out(s, half, on_vector):
+            dst = z[s][:, half * HALF : (half + 1) * HALF]
+            if on_vector:
+                nc.vector.tensor_scalar_max(dst, banks[2 * s + half][:, 0:HALF], 0.0)
+            else:
+                nc.scalar.activation(dst, banks[2 * s + half][:, 0:HALF], RELU)
+
+        low, high, both = slice(0, 8), slice(8, 16), slice(0, 16)
+        cast_w1(0, low, True)
+        cast_w1(0, high, False)
+        cast_w1(1, both, False)
+        cast_w1(3, both, False)
+        cast_w1(2, low, True)
+        quant_w1(0)
+        cast_w1(2, high, True)
+        quant_w1(1)
+        quant_w1(2)
+        quant_w1(3)
+        for s, half in ((0, 0), (0, 1), (1, 0), (1, 1), (2, 0), (2, 1), (3, 0), (3, 1)):
+            layer1(s, half)
+        for s, half in ((0, 0), (0, 1), (2, 0), (2, 1), (3, 0), (3, 1)):
+            relu_out(s, half, False)
+        relu_out(1, 0, True)
+        relu_out(1, 1, True)
+
+        w2_g = keep.tile([P, PACK, P, PACK], BF16, name="w2_g", align_bytes=64)
+        w2_c = keep.tile([P, N], U32, name="w2_c", align_bytes=64)
+        w2_s = keep.tile([P, N], U8, name="w2_s", align_bytes=64)
+        for piece in range(4):
+            ms = slice(32 * piece, 32 * piece + 32)
+            nc.scalar.activation(
+                w2_g[:].rearrange("p t m s -> p m s t")[:, ms],
+                w2_raw[:].rearrange("p s (m t) -> p m s t", t=PACK)[:, ms],
+                COPY,
+            )
+
+        planes = keep.tile([P, PACK, S], BF16, name="planes", tag="w2_then_planes", align_bytes=64)
+
+        def gather(s):
+            nc.vector.tensor_copy(picked[s][:], z[s][:].indirect(give_t[:]))
+
+        def scatter(s):
+            nc.vector.tensor_copy(z[s][:].indirect(take_t[:]), picked[s][:])
+
+        def quant_w2(t0, t1):
+            nc.vector.quantize_mx(
+                out=w2_c[:, t0 * P : t1 * P].bitcast(FP8X4), scales=w2_s[:, t0 * P : t1 * P],
+                in_=w2_g[:, t0:t1].rearrange("p t m s -> p (t m s)"),
+            )
+
+        gather(0)
+        gather(1)
+        scatter(0)
+        gather(2)
+        scatter(1)
+        gather(3)
+        scatter(2)
+        scatter(3)
+        for s in range(3):
+            nc.scalar.copy(planes[:, s, :], z[s][:])
+        quant_w2(0, 2)
+        quant_w2(2, 4)
+        nc.scalar.copy(planes[:, 3, 0:HALF], z[3][:, 0:HALF])
+        nc.scalar.copy(planes[:, 3, HALF:S], z[3][:, HALF:S])
+
+        chunks = S // CHUNK
+        z_g = [keep.tile([P, CHUNK * PACK], BF16, name=f"z_g{c}", align_bytes=64) for c in range(chunks)]
+        z_c = [keep.tile([P, CHUNK], U32, name=f"z_c{c}", align_bytes=64) for c in range(chunks)]
+        z_s = [keep.tile([P, CHUNK], U8, name=f"z_s{c}", align_bytes=64) for c in range(chunks)]
+        y = [keep.tile([P, PACK, CHUNK], F32, name=f"y{c}", align_bytes=64) for c in range(chunks)]
+        y_g = [keep.tile([P, HALF * PACK], BF16, name=f"y_g{c}", align_bytes=64) for c in range(2)]
+        y_c = keep.tile([P, S], U32, name="y_c", align_bytes=64)
+        y_s = keep.tile([P, S], U8, name="y_s", align_bytes=64)
+        out_rows = out_0.rearrange("(p t) c -> p t c", t=PACK)
+        out_words = out_1[0].rearrange("p n t -> p (n t)").bitcast(I32)
+
+        def weave_z(c, engine_copy):
+            cols = slice(c * CHUNK, (c + 1) * CHUNK)
+            engine_copy(
+                z_g[c][:].rearrange("p (a i s) -> p a s i", i=8, s=PACK),
+                planes[:, :, cols].rearrange("p s (a i) -> p a s i", i=8),
+            )
+
+        def y_bank(c, t):
+            if c == -1 and t >= 2:
+                return banks[4][:, (t - 2) * CHUNK : (t - 1) * CHUNK]
+            return banks[c][:, t * CHUNK : (t + 1) * CHUNK]
+
+        def layer2(c):
+            nc.vector.quantize_mx(out=z_c[c][:].bitcast(FP8X4), scales=z_s[c][:], in_=z_g[c][:])
+            for t in range(PACK):
+                nc.tensor.matmul_mx(
+                    out=y_bank(c, t),
+                    lhsT=w2_c[:, t * P : (t + 1) * P].bitcast(FP8X4), lhsT_scale=w2_s[:, t * P : (t + 1) * P],
+                    rhs=z_c[c][:].bitcast(FP8X4), rhs_scale=z_s[c][:], start=True, stop=True,
+                )
+            cols = slice(c * CHUNK, (c + 1) * CHUNK)
+            if c == -1:
+                nc.scalar.copy(y[c][:, 0:2].rearrange("p t c -> p (t c)"), banks[c][:, 0:HALF])
+                nc.vector.tensor_copy(y[c][:, 2:4].rearrange("p t c -> p (t c)"), banks[4][:, 0:HALF])
+            else:
+                nc.scalar.copy(y[c][:].rearrange("p t c -> p (t c)"), banks[c][:])
+            nc.sync.dma_start(out_rows[:, :, cols], y[c][:])
+
+        def weave_y(c):
+            nc.vector.tensor_copy(
+                y_g[c // 2][:, (c % 2) * CHUNK * PACK : (c % 2 + 1) * CHUNK * PACK].rearrange("p (a i t) -> p a t i", i=8, t=PACK),
+                y[c][:].rearrange("p t (a i) -> p a t i", i=8),
+            )
+
+        def quant_y(c):
+            cols = slice(c * HALF, (c + 1) * HALF)
+            nc.vector.quantize_mx(out=y_c[:, cols].bitcast(FP8X4), scales=y_s[:, cols], in_=y_g[c][:])
+
+        weave_z(0, nc.vector.tensor_copy)
+        weave_z(1, nc.scalar.copy)
+        weave_z(2, nc.scalar.copy)
+        layer2(0)
+        layer2(1)
+        weave_z(3, nc.vector.tensor_copy)
+        layer2(2)
+        layer2(3)
+        weave_y(0)
+        weave_y(1)
+        weave_y(2)
+        quant_y(0)
+        nc.sync.dma_start(out_words[:, 0:HALF], y_c[:, 0:HALF].bitcast(I32))
+        weave_y(3)
+        quant_y(1)
+        nc.sync.dma_start(out_words[:, HALF:S], y_c[:, HALF:S].bitcast(I32))
+        for q in range(4):
+            queue = nc.sync if q % 2 == 0 else nc.scalar
+            queue.dma_start(out_2[0, 4 * q : 4 * q + 4, :].bitcast(I32), y_s[32 * q : 32 * q + 4, :].bitcast(I32))

@@ -21,7 +21,8 @@ N = 512
 V = 128
 CHUNK = 128
 HALF = 256
-LAST = 3
+Z_SPLIT = 144
+Y_SPLIT = 128
 FLOPS = 2 * 2 * 512 * 512 * 512
 
 
@@ -41,28 +42,27 @@ def tile_picked_ycutmix_relu_po_kernel(
         xw = keep.tile([P, T], I32, name="xw", align_bytes=64)
         xs = keep.tile([P, T], U8, name="xs", align_bytes=64)
         w1_raw = keep.tile([P, PACK, H], F32, name="w1_raw", align_bytes=64)
-        w2_raw = keep.tile([P, PACK, N], F32, name="w2_raw", tag="w2_then_planes", align_bytes=64)
+        w2_raw = keep.tile([P, PACK, N], F32, name="w2_raw", tag="w2_then_z", align_bytes=64)
 
         nc.vector.memset(xs[:].bitcast(I32), 0)
         warm = keep.tile([P, 2], F32, name="warm")
         nc.gpsimd.memset(warm[:, 0:1], 0.0)
         nc.scalar.activation(warm[:, 1:2], warm[:, 0:1], RELU)
+        w1_rows = w1.rearrange("(p j) c -> p j c", j=PACK)
         nc.sync.dma_start(offs_t[:], offs)
-        nc.sync.dma_start(give_t[:], give)
-        nc.sync.dma_start(xw[:], x_words[0].rearrange("p n t -> p (n t)").bitcast(I32))
+        nc.sync.dma_start(w1_raw[:, 0:2], w1_rows[:, 0:2])
         for q in range(4):
             nc.sync.dma_start(xs[32 * q : 32 * q + 4, :].bitcast(I32), x_scales[0, 4 * q : 4 * q + 4, :].bitcast(I32))
-        w1_rows = w1.rearrange("(p j) c -> p j c", j=PACK)
-        nc.sync.dma_start(w1_raw[:, 0:2], w1_rows[:, 0:2])
         nc.sync.dma_start(w1_raw[:, 2:4], w1_rows[:, 2:4])
+        nc.sync.dma_start(xw[:], x_words[0].rearrange("p n t -> p (n t)").bitcast(I32))
+        nc.sync.dma_start(give_t[:], give)
         nc.sync.dma_start(take_t[:], take)
         w2_rows = w2.rearrange("(b s r) n -> s b r n", s=PACK, r=8)
         for s in range(PACK):
             nc.sync.dma_start(w2_raw[:, s, :], w2_rows[s])
 
-        xq_w = keep.tile([P, S], U32, name="xq_w", align_bytes=64)
+        xq_w = [keep.tile([P, HALF], U32, name=f"xq_w{h}", align_bytes=64) for h in range(2)]
         xq_s = keep.tile([P, S], U8, name="xq_s", align_bytes=64)
-        nc.vector.tensor_copy(xq_w[:], xw[:].bitcast(U32).indirect(offs_t[:]))
         nc.vector.tensor_copy(xq_s[:], xs[:].indirect(offs_t[:]))
 
         w1_view = w1_raw[:].rearrange("p j (b s r) -> p s b j r", s=PACK, r=8)
@@ -87,7 +87,7 @@ def tile_picked_ycutmix_relu_po_kernel(
             cols = slice(half * HALF, (half + 1) * HALF)
             nc.tensor.matmul_mx(
                 out=banks[2 * s + half][:, 0:HALF], lhsT=w1_c[s][:].bitcast(FP8X4), lhsT_scale=w1_s[s][:],
-                rhs=xq_w[:, cols].bitcast(FP8X4), rhs_scale=xq_s[:, cols], start=True, stop=True,
+                rhs=xq_w[half][:].bitcast(FP8X4), rhs_scale=xq_s[:, cols], start=True, stop=True,
             )
 
         def relu_out(s, half, on_vector):
@@ -97,18 +97,18 @@ def tile_picked_ycutmix_relu_po_kernel(
             else:
                 nc.scalar.activation(dst, banks[2 * s + half][:, 0:HALF], RELU)
 
-        low, high, both = slice(0, 8), slice(8, 16), slice(0, 16)
-        cast_w1(0, low, True)
-        cast_w1(0, high, False)
-        cast_w1(1, both, False)
-        cast_w1(3, both, False)
-        cast_w1(2, low, True)
+        both = slice(0, 16)
+        cast_w1(0, both, True)
+        for s in range(1, PACK):
+            cast_w1(s, both, False)
         quant_w1(0)
-        cast_w1(2, high, True)
         quant_w1(1)
+        for half in range(2):
+            picks = offs_t[:, half * HALF // 16 : (half + 1) * HALF // 16]
+            nc.vector.tensor_copy(xq_w[half][:], xw[:].bitcast(U32).indirect(picks))
         quant_w1(2)
         quant_w1(3)
-        for s, half in ((0, 0), (0, 1), (1, 0), (1, 1), (2, 0), (2, 1), (3, 0), (3, 1)):
+        for s, half in ((0, 0), (1, 0), (0, 1), (1, 1), (2, 0), (2, 1), (3, 0), (3, 1)):
             layer1(s, half)
         for s, half in ((0, 0), (0, 1), (2, 0), (2, 1), (3, 0), (3, 1)):
             relu_out(s, half, False)
@@ -126,7 +126,7 @@ def tile_picked_ycutmix_relu_po_kernel(
                 COPY,
             )
 
-        planes = keep.tile([P, PACK, S], BF16, name="planes", tag="w2_then_planes", align_bytes=64)
+        z_all = keep.tile([P, PACK, S], F32, name="z_all", tag="w2_then_z", align_bytes=64)
 
         def gather(s):
             nc.vector.tensor_copy(picked[s][:], z[s][:].indirect(give_t[:]))
@@ -143,83 +143,79 @@ def tile_picked_ycutmix_relu_po_kernel(
         gather(0)
         gather(1)
         scatter(0)
-        gather(2)
+        nc.scalar.copy(z_all[:, 0, :], z[0][:])
         scatter(1)
+        nc.scalar.copy(z_all[:, 1, :], z[1][:])
+        gather(2)
         gather(3)
         scatter(2)
+        nc.scalar.copy(z_all[:, 2, :], z[2][:])
         scatter(3)
-        for s in range(3):
-            nc.scalar.copy(planes[:, s, :], z[s][:])
         quant_w2(0, 2)
         quant_w2(2, 4)
-        nc.scalar.copy(planes[:, 3, 0:HALF], z[3][:, 0:HALF])
-        nc.scalar.copy(planes[:, 3, HALF:S], z[3][:, HALF:S])
 
-        chunks = S // CHUNK
-        z_g = [keep.tile([P, CHUNK * PACK], BF16, name=f"z_g{c}", align_bytes=64) for c in range(chunks)]
-        z_c = [keep.tile([P, CHUNK], U32, name=f"z_c{c}", align_bytes=64) for c in range(chunks)]
-        z_s = [keep.tile([P, CHUNK], U8, name=f"z_s{c}", align_bytes=64) for c in range(chunks)]
-        y = [keep.tile([P, PACK, CHUNK], F32, name=f"y{c}", align_bytes=64) for c in range(chunks)]
-        y_g = [keep.tile([P, HALF * PACK], BF16, name=f"y_g{c}", align_bytes=64) for c in range(2)]
+        spans = ((0, CHUNK), (CHUNK, HALF), (HALF, S))
+        z_g = [keep.tile([P, (b - a) * PACK], BF16, name=f"z_g{a}", align_bytes=64) for a, b in spans]
+        z_c = [keep.tile([P, b - a], U32, name=f"z_c{a}", align_bytes=64) for a, b in spans]
+        z_s = [keep.tile([P, b - a], U8, name=f"z_s{a}", align_bytes=64) for a, b in spans]
+        y = [keep.tile([P, PACK, HALF], F32, name=f"y{h}", align_bytes=64) for h in range(2)]
+        y_g = [keep.tile([P, HALF * PACK], BF16, name=f"y_g{h}", align_bytes=64) for h in range(2)]
         y_c = keep.tile([P, S], U32, name="y_c", align_bytes=64)
         y_s = keep.tile([P, S], U8, name="y_s", align_bytes=64)
         out_rows = out_0.rearrange("(p t) c -> p t c", t=PACK)
         out_words = out_1[0].rearrange("p n t -> p (n t)").bitcast(I32)
 
-        def weave_z(c, engine_copy):
-            cols = slice(c * CHUNK, (c + 1) * CHUNK)
-            engine_copy(
-                z_g[c][:].rearrange("p (a i s) -> p a s i", i=8, s=PACK),
-                planes[:, :, cols].rearrange("p s (a i) -> p a s i", i=8),
+        def weave(copy, grouped, rows, first, last):
+            copy(
+                grouped[:, 0 : (last - first) * PACK].rearrange("p (a i s) -> p a s i", i=4, s=PACK),
+                rows[:, :, first:last].rearrange("p s (a i) -> p a s i", i=4),
             )
 
-        def y_bank(c, t):
-            if c == -1 and t >= 2:
-                return banks[4][:, (t - 2) * CHUNK : (t - 1) * CHUNK]
-            return banks[c][:, t * CHUNK : (t + 1) * CHUNK]
+        def quant_z(h):
+            nc.vector.quantize_mx(out=z_c[h][:].bitcast(FP8X4), scales=z_s[h][:], in_=z_g[h][:])
 
-        def layer2(c):
-            nc.vector.quantize_mx(out=z_c[c][:].bitcast(FP8X4), scales=z_s[c][:], in_=z_g[c][:])
+        def layer2(span, t, bank):
+            nc.tensor.matmul_mx(
+                out=bank,
+                lhsT=w2_c[:, t * P : (t + 1) * P].bitcast(FP8X4), lhsT_scale=w2_s[:, t * P : (t + 1) * P],
+                rhs=z_c[span][:].bitcast(FP8X4), rhs_scale=z_s[span][:], start=True, stop=True,
+            )
+
+        def store_y(h, t):
+            nc.sync.dma_start(out_rows[:, t : t + 2, h * HALF : (h + 1) * HALF], y[h][:, t : t + 2, :])
+
+        def quant_y(h):
+            cols = slice(h * HALF, (h + 1) * HALF)
+            nc.vector.quantize_mx(out=y_c[:, cols].bitcast(FP8X4), scales=y_s[:, cols], in_=y_g[h][:])
+            nc.sync.dma_start(out_words[:, cols], y_c[:, cols].bitcast(I32))
+
+        on_vector, on_scalar = nc.vector.tensor_copy, nc.scalar.copy
+        on_scalar(z_all[:, 3, 0:HALF], z[3][:, 0:HALF])
+        weave(on_vector, z_g[0][:], z_all[:], 0, CHUNK)
+        on_vector(z_all[:, 3, HALF:S], z[3][:, HALF:S])
+        weave(on_scalar, z_g[1][:], z_all[:], CHUNK, HALF)
+        quant_z(0)
+        quant_z(1)
+        weave(on_vector, z_g[2][:], z_all[:], HALF, HALF + Z_SPLIT)
+        weave(on_scalar, z_g[2][:, Z_SPLIT * PACK :], z_all[:], HALF + Z_SPLIT, S)
+        quant_z(2)
+        for c in range(2):
             for t in range(PACK):
-                nc.tensor.matmul_mx(
-                    out=y_bank(c, t),
-                    lhsT=w2_c[:, t * P : (t + 1) * P].bitcast(FP8X4), lhsT_scale=w2_s[:, t * P : (t + 1) * P],
-                    rhs=z_c[c][:].bitcast(FP8X4), rhs_scale=z_s[c][:], start=True, stop=True,
-                )
-            cols = slice(c * CHUNK, (c + 1) * CHUNK)
-            if c == -1:
-                nc.scalar.copy(y[c][:, 0:2].rearrange("p t c -> p (t c)"), banks[c][:, 0:HALF])
-                nc.vector.tensor_copy(y[c][:, 2:4].rearrange("p t c -> p (t c)"), banks[4][:, 0:HALF])
-            else:
-                nc.scalar.copy(y[c][:].rearrange("p t c -> p (t c)"), banks[c][:])
-            nc.sync.dma_start(out_rows[:, :, cols], y[c][:])
-
-        def weave_y(c):
-            nc.vector.tensor_copy(
-                y_g[c // 2][:, (c % 2) * CHUNK * PACK : (c % 2 + 1) * CHUNK * PACK].rearrange("p (a i t) -> p a t i", i=8, t=PACK),
-                y[c][:].rearrange("p t (a i) -> p a t i", i=8),
-            )
-
-        def quant_y(c):
-            cols = slice(c * HALF, (c + 1) * HALF)
-            nc.vector.quantize_mx(out=y_c[:, cols].bitcast(FP8X4), scales=y_s[:, cols], in_=y_g[c][:])
-
-        weave_z(0, nc.vector.tensor_copy)
-        weave_z(1, nc.scalar.copy)
-        weave_z(2, nc.scalar.copy)
-        layer2(0)
-        layer2(1)
-        weave_z(3, nc.vector.tensor_copy)
-        layer2(2)
-        layer2(3)
-        weave_y(0)
-        weave_y(1)
-        weave_y(2)
+                layer2(c, t, banks[c][:, t * CHUNK : (t + 1) * CHUNK])
+            on_vector(y[0][:, :, c * CHUNK : (c + 1) * CHUNK], banks[c][:].rearrange("p (t c) -> p t c", t=PACK))
+        store_y(0, 0)
+        store_y(0, 2)
+        for t in range(PACK):
+            layer2(2, t, banks[4 + t][:, 0:HALF])
+            on_scalar(y[1][:, t, :], banks[4 + t][:, 0:HALF])
+            if t % 2 == 1:
+                store_y(1, t - 1)
+        for c in range(2):
+            weave(on_vector, y_g[0][:, c * CHUNK * PACK :], y[0][:], c * CHUNK, (c + 1) * CHUNK)
         quant_y(0)
-        nc.sync.dma_start(out_words[:, 0:HALF], y_c[:, 0:HALF].bitcast(I32))
-        weave_y(3)
+        weave(on_vector, y_g[1][:], y[1][:], 0, Y_SPLIT)
+        weave(on_scalar, y_g[1][:, Y_SPLIT * PACK :], y[1][:], Y_SPLIT, HALF)
         quant_y(1)
-        nc.sync.dma_start(out_words[:, HALF:S], y_c[:, HALF:S].bitcast(I32))
         for q in range(4):
             queue = nc.sync if q % 2 == 0 else nc.scalar
             queue.dma_start(out_2[0, 4 * q : 4 * q + 4, :].bitcast(I32), y_s[32 * q : 32 * q + 4, :].bitcast(I32))

@@ -21,7 +21,7 @@ N = 512
 V = 128
 CHUNK = 128
 HALF = 256
-Z_SPLIT = 144
+Z_SPLIT = 128
 Y_SPLIT = 128
 FLOPS = 2 * 2 * 512 * 512 * 512
 
@@ -181,8 +181,8 @@ def tile_picked_ycutmix_relu_po_kernel(
                 rhs=z_c[span][:].bitcast(FP8X4), rhs_scale=z_s[span][:], start=True, stop=True,
             )
 
-        def store_y(h, t):
-            nc.sync.dma_start(out_rows[:, t : t + 2, h * HALF : (h + 1) * HALF], y[h][:, t : t + 2, :])
+        def store_y(h, t, count):
+            nc.sync.dma_start(out_rows[:, t : t + count, h * HALF : (h + 1) * HALF], y[h][:, t : t + count, :])
 
         def quant_y(h):
             cols = slice(h * HALF, (h + 1) * HALF)
@@ -191,31 +191,29 @@ def tile_picked_ycutmix_relu_po_kernel(
 
         on_vector, on_scalar = nc.vector.tensor_copy, nc.scalar.copy
         on_scalar(z_all[:, 3, 0:HALF], z[3][:, 0:HALF])
+        on_scalar(z_all[:, 3, HALF:S], z[3][:, HALF:S])
         weave(on_vector, z_g[0][:], z_all[:], 0, CHUNK)
-        on_vector(z_all[:, 3, HALF:S], z[3][:, HALF:S])
         weave(on_scalar, z_g[1][:], z_all[:], CHUNK, HALF)
-        quant_z(0)
-        quant_z(1)
         weave(on_vector, z_g[2][:], z_all[:], HALF, HALF + Z_SPLIT)
         weave(on_scalar, z_g[2][:, Z_SPLIT * PACK :], z_all[:], HALF + Z_SPLIT, S)
+        quant_z(0)
+        quant_z(1)
         quant_z(2)
         for c in range(2):
             for t in range(PACK):
-                layer2(c, t, banks[c][:, t * CHUNK : (t + 1) * CHUNK])
-            on_vector(y[0][:, :, c * CHUNK : (c + 1) * CHUNK], banks[c][:].rearrange("p (t c) -> p t c", t=PACK))
-        store_y(0, 0)
-        store_y(0, 2)
+                layer2(c, t, banks[t][:, c * CHUNK : (c + 1) * CHUNK])
+        for t in range(PACK):
+            (on_scalar if t % 2 == 0 else on_vector)(y[0][:, t, :], banks[t][:, 0:HALF])
+            store_y(0, t, 1)
         for t in range(PACK):
             layer2(2, t, banks[4 + t][:, 0:HALF])
             on_scalar(y[1][:, t, :], banks[4 + t][:, 0:HALF])
             if t % 2 == 1:
-                store_y(1, t - 1)
-        for c in range(2):
-            weave(on_vector, y_g[0][:, c * CHUNK * PACK :], y[0][:], c * CHUNK, (c + 1) * CHUNK)
+                store_y(1, t - 1, 2)
+        weave(on_vector, y_g[0][:], y[0][:], 0, HALF)
         quant_y(0)
         weave(on_vector, y_g[1][:], y[1][:], 0, Y_SPLIT)
         weave(on_scalar, y_g[1][:, Y_SPLIT * PACK :], y[1][:], Y_SPLIT, HALF)
         quant_y(1)
         for q in range(4):
-            queue = nc.sync if q % 2 == 0 else nc.scalar
-            queue.dma_start(out_2[0, 4 * q : 4 * q + 4, :].bitcast(I32), y_s[32 * q : 32 * q + 4, :].bitcast(I32))
+            nc.sync.dma_start(out_2[0, 4 * q : 4 * q + 4, :].bitcast(I32), y_s[32 * q : 32 * q + 4, :].bitcast(I32))

@@ -10,7 +10,7 @@ U16 = mybir.dt.uint16
 U8 = mybir.dt.uint8
 FP8X4 = mybir.dt.float8_e4m3fn_x4
 RELU = mybir.ActivationFunctionType.Relu
-COPY = mybir.ActivationFunctionType.Copy
+IDENTITY = mybir.ActivationFunctionType.Identity
 
 P = 128
 PACK = 4
@@ -19,10 +19,11 @@ S = 512
 H = 512
 N = 512
 V = 128
-CHUNK = 128
 HALF = 256
-Z_SPLIT = 128
-Y_SPLIT = 128
+CHUNK = 128
+SPARE = 8
+Z_PIECE = 88
+Y_SPLIT = 88
 FLOPS = 2 * 2 * 512 * 512 * 512
 
 
@@ -41,92 +42,86 @@ def tile_picked_ycutmix_relu_po_kernel(
 
         xw = keep.tile([P, T], I32, name="xw", align_bytes=64)
         xs = keep.tile([P, T], U8, name="xs", align_bytes=64)
-        w1_raw = keep.tile([P, PACK, H], F32, name="w1_raw", align_bytes=64)
-        w2_raw = keep.tile([P, PACK, N], F32, name="w2_raw", tag="w2_then_z", align_bytes=64)
+        w1_raw = [keep.tile([P, PACK, HALF], F32, name=f"w1_raw{h}", align_bytes=64) for h in range(2)]
+        w2_raw = keep.tile([P, PACK, N], F32, name="w2_raw", align_bytes=64)
+        z_half = [keep.tile([P, PACK, HALF], F32, name=f"z_half{h}", align_bytes=64) for h in range(2)]
 
         nc.vector.memset(xs[:].bitcast(I32), 0)
         warm = keep.tile([P, 2], F32, name="warm")
         nc.gpsimd.memset(warm[:, 0:1], 0.0)
         nc.scalar.activation(warm[:, 1:2], warm[:, 0:1], RELU)
         w1_rows = w1.rearrange("(p j) c -> p j c", j=PACK)
+        nc.sync.dma_start(w1_raw[0][:], w1_rows[:, :, 0:HALF])
         nc.sync.dma_start(offs_t[:], offs)
-        nc.sync.dma_start(w1_raw[:, 0:2], w1_rows[:, 0:2])
         for q in range(4):
             nc.sync.dma_start(xs[32 * q : 32 * q + 4, :].bitcast(I32), x_scales[0, 4 * q : 4 * q + 4, :].bitcast(I32))
-        nc.sync.dma_start(w1_raw[:, 2:4], w1_rows[:, 2:4])
         nc.sync.dma_start(xw[:], x_words[0].rearrange("p n t -> p (n t)").bitcast(I32))
+        nc.sync.dma_start(w1_raw[1][:], w1_rows[:, :, HALF:H])
         nc.sync.dma_start(give_t[:], give)
         nc.sync.dma_start(take_t[:], take)
         w2_rows = w2.rearrange("(b s r) n -> s b r n", s=PACK, r=8)
         for s in range(PACK):
             nc.sync.dma_start(w2_raw[:, s, :], w2_rows[s])
 
-        xq_w = [keep.tile([P, HALF], U32, name=f"xq_w{h}", align_bytes=64) for h in range(2)]
+        xq_w = keep.tile([P, S], U32, name="xq_w", align_bytes=64)
         xq_s = keep.tile([P, S], U8, name="xq_s", align_bytes=64)
         nc.vector.tensor_copy(xq_s[:], xs[:].indirect(offs_t[:]))
+        nc.vector.tensor_copy(xq_w[:], xw[:].bitcast(U32).indirect(offs_t[:]))
 
-        w1_view = w1_raw[:].rearrange("p j (b s r) -> p s b j r", s=PACK, r=8)
         w1_g = [keep.tile([P, P * PACK], BF16, name=f"w1_g{s}", align_bytes=64) for s in range(PACK)]
         w1_c = [keep.tile([P, P], U32, name=f"w1_c{s}", align_bytes=64) for s in range(PACK)]
         w1_s = [keep.tile([P, P], U8, name=f"w1_s{s}", align_bytes=64) for s in range(PACK)]
         banks = [psum.tile([P, 512], F32, name=f"bank{b}") for b in range(8)]
-        z = [keep.tile([P, S], F32, name=f"z{s}", align_bytes=64) for s in range(PACK)]
+        z = [keep.tile([P, S + SPARE], F32, name=f"z{s}", align_bytes=64) for s in range(PACK)]
+        for s in range(PACK):
+            nc.gpsimd.memset(z[s][:, S : S + SPARE], 0.0)
         picked = [keep.tile([P, V], F32, name=f"picked{s}", align_bytes=64) for s in range(PACK)]
+        on_vector, on_scalar = nc.vector.tensor_copy, nc.scalar.copy
 
-        def cast_w1(s, blocks, on_vector):
-            dst = w1_g[s][:].rearrange("p (b r j) -> p b j r", r=8, j=PACK)[:, blocks]
-            if on_vector:
-                nc.vector.tensor_copy(dst, w1_view[:, s, blocks])
-            else:
-                nc.scalar.activation(dst, w1_view[:, s, blocks], COPY)
+        def cast_w1(copy, s, h):
+            src = w1_raw[h][:].rearrange("p j (b s r) -> p s b j r", s=PACK, r=8)[:, s]
+            copy(w1_g[s][:, h * HALF : (h + 1) * HALF].rearrange("p (b r j) -> p b j r", r=8, j=PACK), src)
 
         def quant_w1(s):
             nc.vector.quantize_mx(out=w1_c[s][:].bitcast(FP8X4), scales=w1_s[s][:], in_=w1_g[s][:])
 
-        def layer1(s, half):
-            cols = slice(half * HALF, (half + 1) * HALF)
+        def layer1(s, first, last, bank, on_vector=False):
             nc.tensor.matmul_mx(
-                out=banks[2 * s + half][:, 0:HALF], lhsT=w1_c[s][:].bitcast(FP8X4), lhsT_scale=w1_s[s][:],
-                rhs=xq_w[half][:].bitcast(FP8X4), rhs_scale=xq_s[:, cols], start=True, stop=True,
+                out=bank[:, 0 : last - first], lhsT=w1_c[s][:].bitcast(FP8X4), lhsT_scale=w1_s[s][:],
+                rhs=xq_w[:, first:last].bitcast(FP8X4), rhs_scale=xq_s[:, first:last], start=True, stop=True,
             )
-
-        def relu_out(s, half, on_vector):
-            dst = z[s][:, half * HALF : (half + 1) * HALF]
             if on_vector:
-                nc.vector.tensor_scalar_max(dst, banks[2 * s + half][:, 0:HALF], 0.0)
-            else:
-                nc.scalar.activation(dst, banks[2 * s + half][:, 0:HALF], RELU)
+                nc.vector.tensor_scalar_max(z[s][:, first:last], bank[:, 0 : last - first], 0.0)
+                return
+            zero = z[s - 1][:, S : S + 1] if s >= 2 else 0.0
+            nc.scalar.activation(z[s][:, first:last], bank[:, 0 : last - first], RELU, bias=zero)
 
-        both = slice(0, 16)
-        cast_w1(0, both, True)
+        for s in range(PACK):
+            cast_w1(on_scalar, s, 0)
+        cast_w1(on_vector, 0, 1)
+        cast_w1(on_scalar, 1, 1)
+        cast_w1(on_vector, 2, 1)
+        cast_w1(on_scalar, 3, 1)
+        for s in range(PACK):
+            quant_w1(s)
+        for c in range(4):
+            layer1(0, c * CHUNK, (c + 1) * CHUNK, banks[c], c % 2 == 1)
         for s in range(1, PACK):
-            cast_w1(s, both, False)
-        quant_w1(0)
-        quant_w1(1)
-        for half in range(2):
-            picks = offs_t[:, half * HALF // 16 : (half + 1) * HALF // 16]
-            nc.vector.tensor_copy(xq_w[half][:], xw[:].bitcast(U32).indirect(picks))
-        quant_w1(2)
-        quant_w1(3)
-        for s, half in ((0, 0), (1, 0), (0, 1), (1, 1), (2, 0), (2, 1), (3, 0), (3, 1)):
-            layer1(s, half)
-        for s, half in ((0, 0), (0, 1), (2, 0), (2, 1), (3, 0), (3, 1)):
-            relu_out(s, half, False)
-        relu_out(1, 0, True)
-        relu_out(1, 1, True)
+            layer1(s, 0, S, banks[3 + s])
 
         w2_g = keep.tile([P, PACK, P, PACK], BF16, name="w2_g", align_bytes=64)
         w2_c = keep.tile([P, N], U32, name="w2_c", align_bytes=64)
         w2_s = keep.tile([P, N], U8, name="w2_s", align_bytes=64)
-        for piece in range(4):
-            ms = slice(32 * piece, 32 * piece + 32)
-            nc.scalar.activation(
-                w2_g[:].rearrange("p t m s -> p m s t")[:, ms],
-                w2_raw[:].rearrange("p s (m t) -> p m s t", t=PACK)[:, ms],
-                COPY,
-            )
-
-        z_all = keep.tile([P, PACK, S], F32, name="z_all", tag="w2_then_z", align_bytes=64)
+        for pair in range(2):
+            ts = slice(2 * pair, 2 * pair + 2)
+            for piece in range(2):
+                ms = slice(64 * piece, 64 * piece + 64)
+                nc.scalar.activation(
+                    w2_g[:].rearrange("p t m s -> p m s t")[:, ms, :, ts],
+                    w2_raw[:].rearrange("p s (m t) -> p m s t", t=PACK)[:, ms, :, ts],
+                    IDENTITY,
+                    bias=z[2 + piece][:, S : S + 1] if pair == 0 else 0.0,
+                )
 
         def gather(s):
             nc.vector.tensor_copy(picked[s][:], z[s][:].indirect(give_t[:]))
@@ -140,26 +135,31 @@ def tile_picked_ycutmix_relu_po_kernel(
                 in_=w2_g[:, t0:t1].rearrange("p t m s -> p (t m s)"),
             )
 
+        def collect(copy, s):
+            for h in range(2):
+                copy(z_half[h][:, s, :], z[s][:, h * HALF : (h + 1) * HALF])
+
         gather(0)
-        gather(1)
         scatter(0)
-        nc.scalar.copy(z_all[:, 0, :], z[0][:])
-        scatter(1)
-        nc.scalar.copy(z_all[:, 1, :], z[1][:])
+        collect(nc.sync.dma_start, 0)
+        gather(1)
         gather(2)
+        scatter(1)
+        collect(nc.sync.dma_start, 1)
         gather(3)
         scatter(2)
-        nc.scalar.copy(z_all[:, 2, :], z[2][:])
+        collect(on_scalar, 2)
         scatter(3)
         quant_w2(0, 2)
         quant_w2(2, 4)
+        collect(on_scalar, 3)
 
-        spans = ((0, CHUNK), (CHUNK, HALF), (HALF, S))
-        z_g = [keep.tile([P, (b - a) * PACK], BF16, name=f"z_g{a}", align_bytes=64) for a, b in spans]
-        z_c = [keep.tile([P, b - a], U32, name=f"z_c{a}", align_bytes=64) for a, b in spans]
-        z_s = [keep.tile([P, b - a], U8, name=f"z_s{a}", align_bytes=64) for a, b in spans]
+        spans = (CHUNK, CHUNK, CHUNK, CHUNK)
+        z_g = [keep.tile([P, n * PACK], BF16, name=f"z_g{c}", align_bytes=64) for c, n in enumerate(spans)]
+        z_c = [keep.tile([P, n], U32, name=f"z_c{c}", align_bytes=64) for c, n in enumerate(spans)]
+        z_s = [keep.tile([P, n], U8, name=f"z_s{c}", align_bytes=64) for c, n in enumerate(spans)]
         y = [keep.tile([P, PACK, HALF], F32, name=f"y{h}", align_bytes=64) for h in range(2)]
-        y_g = [keep.tile([P, HALF * PACK], BF16, name=f"y_g{h}", align_bytes=64) for h in range(2)]
+        y_g = [keep.tile([P, CHUNK * PACK], BF16, name=f"y_g{c}", align_bytes=64) for c in range(4)]
         y_c = keep.tile([P, S], U32, name="y_c", align_bytes=64)
         y_s = keep.tile([P, S], U8, name="y_s", align_bytes=64)
         out_rows = out_0.rearrange("(p t) c -> p t c", t=PACK)
@@ -174,46 +174,57 @@ def tile_picked_ycutmix_relu_po_kernel(
         def quant_z(h):
             nc.vector.quantize_mx(out=z_c[h][:].bitcast(FP8X4), scales=z_s[h][:], in_=z_g[h][:])
 
-        def layer2(span, t, bank):
+        def layer2(h, t, bank):
             nc.tensor.matmul_mx(
                 out=bank,
                 lhsT=w2_c[:, t * P : (t + 1) * P].bitcast(FP8X4), lhsT_scale=w2_s[:, t * P : (t + 1) * P],
-                rhs=z_c[span][:].bitcast(FP8X4), rhs_scale=z_s[span][:], start=True, stop=True,
+                rhs=z_c[h][:].bitcast(FP8X4), rhs_scale=z_s[h][:], start=True, stop=True,
             )
 
         def store_y(h, t, count):
             nc.sync.dma_start(out_rows[:, t : t + count, h * HALF : (h + 1) * HALF], y[h][:, t : t + count, :])
 
-        def quant_y(h):
+        def quant_y(c):
+            cols = slice(c * CHUNK, (c + 1) * CHUNK)
+            nc.vector.quantize_mx(out=y_c[:, cols].bitcast(FP8X4), scales=y_s[:, cols], in_=y_g[c][:])
+
+        def store_words(h):
             cols = slice(h * HALF, (h + 1) * HALF)
-            nc.vector.quantize_mx(out=y_c[:, cols].bitcast(FP8X4), scales=y_s[:, cols], in_=y_g[h][:])
             nc.sync.dma_start(out_words[:, cols], y_c[:, cols].bitcast(I32))
 
-        on_vector, on_scalar = nc.vector.tensor_copy, nc.scalar.copy
-        on_scalar(z_all[:, 3, 0:HALF], z[3][:, 0:HALF])
-        on_scalar(z_all[:, 3, HALF:S], z[3][:, HALF:S])
-        weave(on_vector, z_g[0][:], z_all[:], 0, CHUNK)
-        weave(on_scalar, z_g[1][:], z_all[:], CHUNK, HALF)
-        weave(on_vector, z_g[2][:], z_all[:], HALF, HALF + Z_SPLIT)
-        weave(on_scalar, z_g[2][:, Z_SPLIT * PACK :], z_all[:], HALF + Z_SPLIT, S)
+        def products(c, copies):
+            first = (c % 2) * CHUNK
+            for t in range(PACK):
+                bank = banks[4 * (c % 2) + t][:, 0:CHUNK]
+                layer2(c, t, bank)
+                copies[t](y[c // 2][:, t, first : first + CHUNK], bank)
+
+        weave(on_vector, z_g[0][:], z_half[0][:], 0, CHUNK)
+        weave(on_scalar, z_g[1][:], z_half[0][:], CHUNK, HALF)
         quant_z(0)
         quant_z(1)
+        weave(on_vector, z_g[2][:], z_half[1][:], 0, CHUNK)
+        weave(on_vector, z_g[3][:], z_half[1][:], CHUNK, HALF)
         quant_z(2)
-        for c in range(2):
-            for t in range(PACK):
-                layer2(c, t, banks[t][:, c * CHUNK : (c + 1) * CHUNK])
+        quant_z(3)
+        products(0, [on_scalar] * 4)
+        weave(on_vector, y_g[0][:], y[0][:], 0, CHUNK)
+        products(1, [on_scalar] * 4)
         for t in range(PACK):
-            (on_scalar if t % 2 == 0 else on_vector)(y[0][:, t, :], banks[t][:, 0:HALF])
             store_y(0, t, 1)
-        for t in range(PACK):
-            layer2(2, t, banks[4 + t][:, 0:HALF])
-            on_scalar(y[1][:, t, :], banks[4 + t][:, 0:HALF])
-            if t % 2 == 1:
-                store_y(1, t - 1, 2)
-        weave(on_vector, y_g[0][:], y[0][:], 0, HALF)
         quant_y(0)
-        weave(on_vector, y_g[1][:], y[1][:], 0, Y_SPLIT)
-        weave(on_scalar, y_g[1][:, Y_SPLIT * PACK :], y[1][:], Y_SPLIT, HALF)
+        weave(on_vector, y_g[1][:], y[0][:], CHUNK, HALF)
+        products(2, [on_scalar] * 4)
         quant_y(1)
+        store_words(0)
+        weave(on_vector, y_g[2][:], y[1][:], 0, CHUNK)
+        products(3, [on_scalar] * 4)
+        store_y(1, 0, 2)
+        store_y(1, 2, 2)
+        quant_y(2)
+        weave(on_vector, y_g[3][:], y[1][:], CHUNK, CHUNK + Y_SPLIT)
+        weave(on_scalar, y_g[3][:, Y_SPLIT * PACK :], y[1][:], CHUNK + Y_SPLIT, HALF)
+        quant_y(3)
+        store_words(1)
         for q in range(4):
             nc.sync.dma_start(out_2[0, 4 * q : 4 * q + 4, :].bitcast(I32), y_s[32 * q : 32 * q + 4, :].bitcast(I32))

@@ -22,8 +22,8 @@ V = 128
 HALF = 256
 CHUNK = 128
 SPARE = 8
-Z_PIECE = 88
-Y_SPLIT = 88
+Z_SPLIT = 64
+Y_SPLIT = 168
 FLOPS = 2 * 2 * 512 * 512 * 512
 
 
@@ -42,7 +42,7 @@ def tile_picked_ycutmix_relu_po_kernel(
 
         xw = keep.tile([P, T], I32, name="xw", align_bytes=64)
         xs = keep.tile([P, T], U8, name="xs", align_bytes=64)
-        w1_raw = [keep.tile([P, PACK, HALF], F32, name=f"w1_raw{h}", align_bytes=64) for h in range(2)]
+        w1_raw = [keep.tile([P, 2, H], F32, name=f"w1_raw{h}", align_bytes=64) for h in range(2)]
         w2_raw = keep.tile([P, PACK, N], F32, name="w2_raw", align_bytes=64)
         z_half = [keep.tile([P, PACK, HALF], F32, name=f"z_half{h}", align_bytes=64) for h in range(2)]
 
@@ -51,12 +51,12 @@ def tile_picked_ycutmix_relu_po_kernel(
         nc.gpsimd.memset(warm[:, 0:1], 0.0)
         nc.scalar.activation(warm[:, 1:2], warm[:, 0:1], RELU)
         w1_rows = w1.rearrange("(p j) c -> p j c", j=PACK)
-        nc.sync.dma_start(w1_raw[0][:], w1_rows[:, :, 0:HALF])
+        nc.sync.dma_start(w1_raw[0][:], w1_rows[:, 0:2])
         nc.sync.dma_start(offs_t[:], offs)
         for q in range(4):
             nc.sync.dma_start(xs[32 * q : 32 * q + 4, :].bitcast(I32), x_scales[0, 4 * q : 4 * q + 4, :].bitcast(I32))
         nc.sync.dma_start(xw[:], x_words[0].rearrange("p n t -> p (n t)").bitcast(I32))
-        nc.sync.dma_start(w1_raw[1][:], w1_rows[:, :, HALF:H])
+        nc.sync.dma_start(w1_raw[1][:], w1_rows[:, 2:4])
         nc.sync.dma_start(give_t[:], give)
         nc.sync.dma_start(take_t[:], take)
         w2_rows = w2.rearrange("(b s r) n -> s b r n", s=PACK, r=8)
@@ -80,7 +80,7 @@ def tile_picked_ycutmix_relu_po_kernel(
 
         def cast_w1(copy, s, h):
             src = w1_raw[h][:].rearrange("p j (b s r) -> p s b j r", s=PACK, r=8)[:, s]
-            copy(w1_g[s][:, h * HALF : (h + 1) * HALF].rearrange("p (b r j) -> p b j r", r=8, j=PACK), src)
+            copy(w1_g[s][:].rearrange("p (b r j) -> p b j r", r=8, j=PACK)[:, :, 2 * h : 2 * h + 2], src)
 
         def quant_w1(s):
             nc.vector.quantize_mx(out=w1_c[s][:].bitcast(FP8X4), scales=w1_s[s][:], in_=w1_g[s][:])
@@ -152,14 +152,15 @@ def tile_picked_ycutmix_relu_po_kernel(
         scatter(3)
         quant_w2(0, 2)
         quant_w2(2, 4)
-        collect(on_scalar, 3)
+        on_scalar(z_half[0][:, 3, 0:CHUNK], z[3][:, 0:CHUNK])
+        on_scalar(z_half[0][:, 3, CHUNK:HALF], z[3][:, CHUNK:HALF])
+        on_scalar(z_half[1][:, 3, :], z[3][:, HALF:S])
 
-        spans = (CHUNK, CHUNK, CHUNK, CHUNK)
-        z_g = [keep.tile([P, n * PACK], BF16, name=f"z_g{c}", align_bytes=64) for c, n in enumerate(spans)]
-        z_c = [keep.tile([P, n], U32, name=f"z_c{c}", align_bytes=64) for c, n in enumerate(spans)]
-        z_s = [keep.tile([P, n], U8, name=f"z_s{c}", align_bytes=64) for c, n in enumerate(spans)]
+        z_g = [keep.tile([P, CHUNK * PACK], BF16, name=f"z_g{c}", align_bytes=64) for c in range(4)]
+        z_c = [keep.tile([P, HALF], U32, name=f"z_c{h}", align_bytes=64) for h in range(2)]
+        z_s = [keep.tile([P, HALF], U8, name=f"z_s{h}", align_bytes=64) for h in range(2)]
         y = [keep.tile([P, PACK, HALF], F32, name=f"y{h}", align_bytes=64) for h in range(2)]
-        y_g = [keep.tile([P, CHUNK * PACK], BF16, name=f"y_g{c}", align_bytes=64) for c in range(4)]
+        y_g = [keep.tile([P, HALF * PACK], BF16, name=f"y_g{h}", align_bytes=64) for h in range(2)]
         y_c = keep.tile([P, S], U32, name="y_c", align_bytes=64)
         y_s = keep.tile([P, S], U8, name="y_s", align_bytes=64)
         out_rows = out_0.rearrange("(p t) c -> p t c", t=PACK)
@@ -171,60 +172,49 @@ def tile_picked_ycutmix_relu_po_kernel(
                 rows[:, :, first:last].rearrange("p s (a i) -> p a s i", i=4),
             )
 
-        def quant_z(h):
-            nc.vector.quantize_mx(out=z_c[h][:].bitcast(FP8X4), scales=z_s[h][:], in_=z_g[h][:])
+        def quant_z(c):
+            cols = slice((c % 2) * CHUNK, (c % 2 + 1) * CHUNK)
+            nc.vector.quantize_mx(out=z_c[c // 2][:, cols].bitcast(FP8X4), scales=z_s[c // 2][:, cols], in_=z_g[c][:])
 
-        def layer2(h, t, bank):
+        def layer2(h, t, first, last, bank):
             nc.tensor.matmul_mx(
-                out=bank,
+                out=bank[:, 0 : last - first],
                 lhsT=w2_c[:, t * P : (t + 1) * P].bitcast(FP8X4), lhsT_scale=w2_s[:, t * P : (t + 1) * P],
-                rhs=z_c[h][:].bitcast(FP8X4), rhs_scale=z_s[h][:], start=True, stop=True,
+                rhs=z_c[h][:, first:last].bitcast(FP8X4), rhs_scale=z_s[h][:, first:last], start=True, stop=True,
             )
+            on_scalar(y[h][:, t, first:last], bank[:, 0 : last - first])
 
         def store_y(h, t, count):
             nc.sync.dma_start(out_rows[:, t : t + count, h * HALF : (h + 1) * HALF], y[h][:, t : t + count, :])
 
-        def quant_y(c):
-            cols = slice(c * CHUNK, (c + 1) * CHUNK)
-            nc.vector.quantize_mx(out=y_c[:, cols].bitcast(FP8X4), scales=y_s[:, cols], in_=y_g[c][:])
-
-        def store_words(h):
+        def quant_y(h):
             cols = slice(h * HALF, (h + 1) * HALF)
+            nc.vector.quantize_mx(out=y_c[:, cols].bitcast(FP8X4), scales=y_s[:, cols], in_=y_g[h][:])
             nc.sync.dma_start(out_words[:, cols], y_c[:, cols].bitcast(I32))
 
-        def products(c, copies):
-            first = (c % 2) * CHUNK
-            for t in range(PACK):
-                bank = banks[4 * (c % 2) + t][:, 0:CHUNK]
-                layer2(c, t, bank)
-                copies[t](y[c // 2][:, t, first : first + CHUNK], bank)
-
         weave(on_vector, z_g[0][:], z_half[0][:], 0, CHUNK)
-        weave(on_scalar, z_g[1][:], z_half[0][:], CHUNK, HALF)
+        weave(on_vector, z_g[1][:], z_half[0][:], CHUNK, CHUNK + Z_SPLIT)
+        weave(on_scalar, z_g[1][:, Z_SPLIT * PACK :], z_half[0][:], CHUNK + Z_SPLIT, HALF)
         quant_z(0)
         quant_z(1)
-        weave(on_vector, z_g[2][:], z_half[1][:], 0, CHUNK)
+        weave(on_scalar, z_g[2][:], z_half[1][:], 0, CHUNK)
         weave(on_vector, z_g[3][:], z_half[1][:], CHUNK, HALF)
         quant_z(2)
         quant_z(3)
-        products(0, [on_scalar] * 4)
-        weave(on_vector, y_g[0][:], y[0][:], 0, CHUNK)
-        products(1, [on_scalar] * 4)
-        for t in range(PACK):
+        layer2(0, 0, 0, CHUNK, banks[0])
+        layer2(0, 0, CHUNK, HALF, banks[1])
+        store_y(0, 0, 1)
+        for t in range(1, PACK):
+            layer2(0, t, 0, HALF, banks[1 + t])
             store_y(0, t, 1)
+        for t in range(PACK):
+            layer2(1, t, 0, HALF, banks[(5 + t) % 8])
+            if t % 2 == 1:
+                store_y(1, t - 1, 2)
+        weave(on_vector, y_g[0][:], y[0][:], 0, HALF)
         quant_y(0)
-        weave(on_vector, y_g[1][:], y[0][:], CHUNK, HALF)
-        products(2, [on_scalar] * 4)
+        weave(on_vector, y_g[1][:], y[1][:], 0, Y_SPLIT)
+        weave(on_scalar, y_g[1][:, Y_SPLIT * PACK :], y[1][:], Y_SPLIT, HALF)
         quant_y(1)
-        store_words(0)
-        weave(on_vector, y_g[2][:], y[1][:], 0, CHUNK)
-        products(3, [on_scalar] * 4)
-        store_y(1, 0, 2)
-        store_y(1, 2, 2)
-        quant_y(2)
-        weave(on_vector, y_g[3][:], y[1][:], CHUNK, CHUNK + Y_SPLIT)
-        weave(on_scalar, y_g[3][:, Y_SPLIT * PACK :], y[1][:], CHUNK + Y_SPLIT, HALF)
-        quant_y(3)
-        store_words(1)
         for q in range(4):
-            nc.sync.dma_start(out_2[0, 4 * q : 4 * q + 4, :].bitcast(I32), y_s[32 * q : 32 * q + 4, :].bitcast(I32))
+            nc.scalar.dma_start(out_2[0, 4 * q : 4 * q + 4, :].bitcast(I32), y_s[32 * q : 32 * q + 4, :].bitcast(I32))

@@ -23,7 +23,7 @@ HALF = 256
 CHUNK = 128
 SPARE = 8
 Z_SPLIT = 64
-Y_SPLIT = 168
+Y_SPLIT = 56
 FLOPS = 2 * 2 * 512 * 512 * 512
 
 
@@ -47,28 +47,23 @@ def tile_picked_ycutmix_relu_po_kernel(
         z_half = [keep.tile([P, PACK, HALF], F32, name=f"z_half{h}", align_bytes=64) for h in range(2)]
 
         nc.vector.memset(xs[:].bitcast(I32), 0)
-        warm = keep.tile([P, 2], F32, name="warm")
-        nc.gpsimd.memset(warm[:, 0:1], 0.0)
-        nc.scalar.activation(warm[:, 1:2], warm[:, 0:1], RELU)
         w1_rows = w1.rearrange("(p j) c -> p j c", j=PACK)
-        nc.sync.dma_start(w1_raw[0][:], w1_rows[:, 0:2])
+        nc.sync.dma_start(xw[:], x_words[0].rearrange("p n t -> p (n t)").bitcast(I32))
         nc.sync.dma_start(offs_t[:], offs)
         for q in range(4):
             nc.sync.dma_start(xs[32 * q : 32 * q + 4, :].bitcast(I32), x_scales[0, 4 * q : 4 * q + 4, :].bitcast(I32))
-        nc.sync.dma_start(xw[:], x_words[0].rearrange("p n t -> p (n t)").bitcast(I32))
+        nc.sync.dma_start(w1_raw[0][:], w1_rows[:, 0:2])
         nc.sync.dma_start(w1_raw[1][:], w1_rows[:, 2:4])
         nc.sync.dma_start(give_t[:], give)
         nc.sync.dma_start(take_t[:], take)
-        w2_rows = w2.rearrange("(b s r) n -> s b r n", s=PACK, r=8)
-        for s in range(PACK):
-            nc.sync.dma_start(w2_raw[:, s, :], w2_rows[s])
+        nc.sync.dma_start(w2_raw[:], w2.rearrange("(p s) n -> p s n", s=PACK))
 
         xq_w = keep.tile([P, S], U32, name="xq_w", align_bytes=64)
         xq_s = keep.tile([P, S], U8, name="xq_s", align_bytes=64)
-        nc.vector.tensor_copy(xq_s[:], xs[:].indirect(offs_t[:]))
         nc.vector.tensor_copy(xq_w[:], xw[:].bitcast(U32).indirect(offs_t[:]))
+        nc.vector.tensor_copy(xq_s[:], xs[:].indirect(offs_t[:]))
 
-        w1_g = [keep.tile([P, P * PACK], BF16, name=f"w1_g{s}", align_bytes=64) for s in range(PACK)]
+        w1_g = keep.tile([P, PACK, P, PACK], BF16, name="w1_g", align_bytes=64)
         w1_c = [keep.tile([P, P], U32, name=f"w1_c{s}", align_bytes=64) for s in range(PACK)]
         w1_s = [keep.tile([P, P], U8, name=f"w1_s{s}", align_bytes=64) for s in range(PACK)]
         banks = [psum.tile([P, 512], F32, name=f"bank{b}") for b in range(8)]
@@ -79,11 +74,11 @@ def tile_picked_ycutmix_relu_po_kernel(
         on_vector, on_scalar = nc.vector.tensor_copy, nc.scalar.copy
 
         def cast_w1(copy, s, h):
-            src = w1_raw[h][:].rearrange("p j (b s r) -> p s b j r", s=PACK, r=8)[:, s]
-            copy(w1_g[s][:].rearrange("p (b r j) -> p b j r", r=8, j=PACK)[:, :, 2 * h : 2 * h + 2], src)
+            src = w1_raw[h][:].rearrange("p j (m s) -> p m j s", s=PACK)[:, :, :, s]
+            copy(w1_g[:].rearrange("p s m j -> p m j s")[:, :, 2 * h : 2 * h + 2, s], src)
 
         def quant_w1(s):
-            nc.vector.quantize_mx(out=w1_c[s][:].bitcast(FP8X4), scales=w1_s[s][:], in_=w1_g[s][:])
+            nc.vector.quantize_mx(out=w1_c[s][:].bitcast(FP8X4), scales=w1_s[s][:], in_=w1_g[:, s].rearrange("p m j -> p (m j)"))
 
         def layer1(s, first, last, bank, on_vector=False):
             nc.tensor.matmul_mx(
@@ -96,16 +91,15 @@ def tile_picked_ycutmix_relu_po_kernel(
             zero = z[s - 1][:, S : S + 1] if s >= 2 else 0.0
             nc.scalar.activation(z[s][:, first:last], bank[:, 0 : last - first], RELU, bias=zero)
 
-        for s in range(PACK):
-            cast_w1(on_scalar, s, 0)
+        cast_w1(on_scalar, slice(0, 2), 0)
+        cast_w1(on_scalar, slice(2, 4), 0)
         cast_w1(on_vector, 0, 1)
-        cast_w1(on_scalar, 1, 1)
-        cast_w1(on_vector, 2, 1)
-        cast_w1(on_scalar, 3, 1)
+        cast_w1(on_vector, 1, 1)
+        cast_w1(on_scalar, slice(2, 4), 1)
         for s in range(PACK):
             quant_w1(s)
         for c in range(4):
-            layer1(0, c * CHUNK, (c + 1) * CHUNK, banks[c], c % 2 == 1)
+            layer1(0, c * CHUNK, (c + 1) * CHUNK, banks[c], c == 3)
         for s in range(1, PACK):
             layer1(s, 0, S, banks[3 + s])
 
@@ -160,7 +154,7 @@ def tile_picked_ycutmix_relu_po_kernel(
         z_c = [keep.tile([P, HALF], U32, name=f"z_c{h}", align_bytes=64) for h in range(2)]
         z_s = [keep.tile([P, HALF], U8, name=f"z_s{h}", align_bytes=64) for h in range(2)]
         y = [keep.tile([P, PACK, HALF], F32, name=f"y{h}", align_bytes=64) for h in range(2)]
-        y_g = [keep.tile([P, HALF * PACK], BF16, name=f"y_g{h}", align_bytes=64) for h in range(2)]
+        y_g = [keep.tile([P, CHUNK * PACK], BF16, name=f"y_g{c}", align_bytes=64) for c in range(4)]
         y_c = keep.tile([P, S], U32, name="y_c", align_bytes=64)
         y_s = keep.tile([P, S], U8, name="y_s", align_bytes=64)
         out_rows = out_0.rearrange("(p t) c -> p t c", t=PACK)
@@ -176,20 +170,23 @@ def tile_picked_ycutmix_relu_po_kernel(
             cols = slice((c % 2) * CHUNK, (c % 2 + 1) * CHUNK)
             nc.vector.quantize_mx(out=z_c[c // 2][:, cols].bitcast(FP8X4), scales=z_s[c // 2][:, cols], in_=z_g[c][:])
 
-        def layer2(h, t, first, last, bank):
+        def layer2(h, t, first, last, bank, copy=on_scalar):
             nc.tensor.matmul_mx(
                 out=bank[:, 0 : last - first],
                 lhsT=w2_c[:, t * P : (t + 1) * P].bitcast(FP8X4), lhsT_scale=w2_s[:, t * P : (t + 1) * P],
                 rhs=z_c[h][:, first:last].bitcast(FP8X4), rhs_scale=z_s[h][:, first:last], start=True, stop=True,
             )
-            on_scalar(y[h][:, t, first:last], bank[:, 0 : last - first])
+            copy(y[h][:, t, first:last], bank[:, 0 : last - first])
 
         def store_y(h, t, count):
             nc.sync.dma_start(out_rows[:, t : t + count, h * HALF : (h + 1) * HALF], y[h][:, t : t + count, :])
 
-        def quant_y(h):
+        def quant_y(c):
+            cols = slice(c * CHUNK, (c + 1) * CHUNK)
+            nc.vector.quantize_mx(out=y_c[:, cols].bitcast(FP8X4), scales=y_s[:, cols], in_=y_g[c][:])
+
+        def store_words(h):
             cols = slice(h * HALF, (h + 1) * HALF)
-            nc.vector.quantize_mx(out=y_c[:, cols].bitcast(FP8X4), scales=y_s[:, cols], in_=y_g[h][:])
             nc.sync.dma_start(out_words[:, cols], y_c[:, cols].bitcast(I32))
 
         weave(on_vector, z_g[0][:], z_half[0][:], 0, CHUNK)
@@ -204,17 +201,30 @@ def tile_picked_ycutmix_relu_po_kernel(
         layer2(0, 0, 0, CHUNK, banks[0])
         layer2(0, 0, CHUNK, HALF, banks[1])
         store_y(0, 0, 1)
-        for t in range(1, PACK):
+        for t in (1, 2):
             layer2(0, t, 0, HALF, banks[1 + t])
             store_y(0, t, 1)
-        for t in range(PACK):
-            layer2(1, t, 0, HALF, banks[(5 + t) % 8])
-            if t % 2 == 1:
-                store_y(1, t - 1, 2)
-        weave(on_vector, y_g[0][:], y[0][:], 0, HALF)
+        layer2(0, 3, 0, CHUNK, banks[4])
+        layer2(0, 3, CHUNK, HALF, banks[5])
+        store_y(0, 3, 1)
+        weave(on_vector, y_g[0][:], y[0][:], 0, CHUNK)
+        weave(on_vector, y_g[1][:], y[0][:], CHUNK, HALF)
         quant_y(0)
-        weave(on_vector, y_g[1][:], y[1][:], 0, Y_SPLIT)
-        weave(on_scalar, y_g[1][:, Y_SPLIT * PACK :], y[1][:], Y_SPLIT, HALF)
         quant_y(1)
+        for t in (0, 1):
+            layer2(1, t, 0, HALF, banks[6 + t])
+        store_y(1, 0, 2)
+        layer2(1, 2, 0, CHUNK, banks[0])
+        layer2(1, 3, 0, CHUNK, banks[1])
+        layer2(1, 2, CHUNK, HALF, banks[2])
+        layer2(1, 3, CHUNK, HALF, banks[5], on_vector)
+        store_y(1, 2, 2)
+        store_words(0)
+        weave(on_vector, y_g[2][:], y[1][:], 0, CHUNK)
+        weave(on_vector, y_g[3][:], y[1][:], CHUNK, CHUNK + Y_SPLIT)
+        weave(on_scalar, y_g[3][:, Y_SPLIT * PACK :], y[1][:], CHUNK + Y_SPLIT, HALF)
+        quant_y(2)
+        quant_y(3)
+        store_words(1)
         for q in range(4):
             nc.scalar.dma_start(out_2[0, 4 * q : 4 * q + 4, :].bitcast(I32), y_s[32 * q : 32 * q + 4, :].bitcast(I32))

@@ -42,66 +42,75 @@ def tile_picked_ycutmix_relu_po_kernel(
 
         xw = keep.tile([P, T], I32, name="xw", align_bytes=64)
         xs = keep.tile([P, T], U8, name="xs", align_bytes=64)
-        w1_raw = [keep.tile([P, 2, H], F32, name=f"w1_raw{h}", align_bytes=64) for h in range(2)]
+        w1_raw = [keep.tile([P, PACK, HALF], F32, name=f"w1_raw{h}", align_bytes=64) for h in range(2)]
         w2_raw = keep.tile([P, PACK, N], F32, name="w2_raw", align_bytes=64)
-        z_half = [keep.tile([P, PACK, HALF], F32, name=f"z_half{h}", align_bytes=64) for h in range(2)]
+        z_all = keep.tile([P, PACK, S], F32, name="z_all", align_bytes=64)
 
         nc.vector.memset(xs[:].bitcast(I32), 0)
         w1_rows = w1.rearrange("(p j) c -> p j c", j=PACK)
-        nc.sync.dma_start(xw[:], x_words[0].rearrange("p n t -> p (n t)").bitcast(I32))
         nc.sync.dma_start(offs_t[:], offs)
+        nc.sync.dma_start(w1_raw[0][:, 0:3], w1_rows[:, 0:3, 0:HALF])
         for q in range(4):
             nc.sync.dma_start(xs[32 * q : 32 * q + 4, :].bitcast(I32), x_scales[0, 4 * q : 4 * q + 4, :].bitcast(I32))
-        nc.sync.dma_start(w1_raw[0][:], w1_rows[:, 0:2])
-        nc.sync.dma_start(w1_raw[1][:], w1_rows[:, 2:4])
+        nc.sync.dma_start(w1_raw[0][:, 3], w1_rows[:, 3, 0:HALF])
+        nc.sync.dma_start(xw[:], x_words[0].rearrange("p n t -> p (n t)").bitcast(I32))
+        nc.sync.dma_start(w1_raw[1][:], w1_rows[:, :, HALF:H])
         nc.sync.dma_start(give_t[:], give)
         nc.sync.dma_start(take_t[:], take)
         nc.sync.dma_start(w2_raw[:], w2.rearrange("(p s) n -> p s n", s=PACK))
 
         xq_w = keep.tile([P, S], U32, name="xq_w", align_bytes=64)
         xq_s = keep.tile([P, S], U8, name="xq_s", align_bytes=64)
-        nc.vector.tensor_copy(xq_w[:], xw[:].bitcast(U32).indirect(offs_t[:]))
         nc.vector.tensor_copy(xq_s[:], xs[:].indirect(offs_t[:]))
 
-        w1_g = keep.tile([P, PACK, P, PACK], BF16, name="w1_g", align_bytes=64)
+        w1_g = [keep.tile([P, 2, P, PACK], BF16, name=f"w1_g{pair}", tag=f"w1_g{pair}", align_bytes=64) for pair in range(2)]
         w1_c = [keep.tile([P, P], U32, name=f"w1_c{s}", align_bytes=64) for s in range(PACK)]
         w1_s = [keep.tile([P, P], U8, name=f"w1_s{s}", align_bytes=64) for s in range(PACK)]
         banks = [psum.tile([P, 512], F32, name=f"bank{b}") for b in range(8)]
-        z = [keep.tile([P, S + SPARE], F32, name=f"z{s}", align_bytes=64) for s in range(PACK)]
-        for s in range(PACK):
+        z = [keep.tile([P, S + (SPARE if s >= 1 else 0)], F32, name=f"z{s}", align_bytes=64) for s in range(PACK)]
+        for s in (1, 2):
             nc.gpsimd.memset(z[s][:, S : S + SPARE], 0.0)
-        picked = [keep.tile([P, V], F32, name=f"picked{s}", align_bytes=64) for s in range(PACK)]
+        nc.scalar.copy(z[3][:, S : S + SPARE], z[2][:, S : S + SPARE])
         on_vector, on_scalar = nc.vector.tensor_copy, nc.scalar.copy
 
-        def cast_w1(copy, s, h):
-            src = w1_raw[h][:].rearrange("p j (m s) -> p m j s", s=PACK)[:, :, :, s]
-            copy(w1_g[:].rearrange("p s m j -> p m j s")[:, :, 2 * h : 2 * h + 2, s], src)
+        def cast_w1(copy, h, pair):
+            src = w1_raw[h][:].rearrange("p j (m s) -> p m j s", s=PACK)[:, :, :, 2 * pair : 2 * pair + 2]
+            if pair == 0:
+                dst = w1_g[0][:, h].rearrange("p (s m) j -> p m j s", s=2)
+            else:
+                dst = w1_g[1][:, :, 64 * h : 64 * h + 64].rearrange("p s m j -> p m j s")
+            copy(dst, src)
+
+        def pick_words(first, last):
+            nc.vector.tensor_copy(xq_w[:, first:last], xw[:].bitcast(U32).indirect(offs_t[:, first // 16 : last // 16]))
 
         def quant_w1(s):
-            nc.vector.quantize_mx(out=w1_c[s][:].bitcast(FP8X4), scales=w1_s[s][:], in_=w1_g[:, s].rearrange("p m j -> p (m j)"))
+            nc.vector.quantize_mx(out=w1_c[s][:].bitcast(FP8X4), scales=w1_s[s][:], in_=w1_g[s // 2][:, s % 2].rearrange("p m j -> p (m j)"))
 
-        def layer1(s, first, last, bank, on_vector=False):
+        def layer1(s, first, last, bank):
             nc.tensor.matmul_mx(
                 out=bank[:, 0 : last - first], lhsT=w1_c[s][:].bitcast(FP8X4), lhsT_scale=w1_s[s][:],
                 rhs=xq_w[:, first:last].bitcast(FP8X4), rhs_scale=xq_s[:, first:last], start=True, stop=True,
             )
-            if on_vector:
-                nc.vector.tensor_scalar_max(z[s][:, first:last], bank[:, 0 : last - first], 0.0)
-                return
             zero = z[s - 1][:, S : S + 1] if s >= 2 else 0.0
             nc.scalar.activation(z[s][:, first:last], bank[:, 0 : last - first], RELU, bias=zero)
 
-        cast_w1(on_scalar, slice(0, 2), 0)
-        cast_w1(on_scalar, slice(2, 4), 0)
-        cast_w1(on_vector, 0, 1)
+        cast_w1(on_scalar, 0, 0)
+        cast_w1(on_scalar, 0, 1)
+        quant_w1(0)
+        pieces = ((0, HALF), (HALF, HALF + CHUNK), (HALF + CHUNK, S))
+        for first, last in pieces:
+            pick_words(first, last)
+        cast_w1(on_vector, 1, 0)
         cast_w1(on_vector, 1, 1)
-        cast_w1(on_scalar, slice(2, 4), 1)
-        for s in range(PACK):
-            quant_w1(s)
-        for c in range(4):
-            layer1(0, c * CHUNK, (c + 1) * CHUNK, banks[c], c == 3)
         for s in range(1, PACK):
-            layer1(s, 0, S, banks[3 + s])
+            quant_w1(s)
+        for c, (first, last) in enumerate(pieces):
+            layer1(0, first, last, banks[c])
+        for h in range(2):
+            layer1(1, h * HALF, (h + 1) * HALF, banks[3 + h])
+        layer1(2, 0, S, banks[5])
+        layer1(3, 0, S, banks[6])
 
         w2_g = keep.tile([P, PACK, P, PACK], BF16, name="w2_g", align_bytes=64)
         w2_c = keep.tile([P, N], U32, name="w2_c", align_bytes=64)
@@ -117,6 +126,11 @@ def tile_picked_ycutmix_relu_po_kernel(
                     bias=z[2 + piece][:, S : S + 1] if pair == 0 else 0.0,
                 )
 
+        picked = [
+            keep.tile([P, V], F32, name=f"picked{s}", tag="w1_g1" if s == 0 else f"picked{s}", align_bytes=64)
+            for s in range(PACK)
+        ]
+
         def gather(s):
             nc.vector.tensor_copy(picked[s][:], z[s][:].indirect(give_t[:]))
 
@@ -129,26 +143,26 @@ def tile_picked_ycutmix_relu_po_kernel(
                 in_=w2_g[:, t0:t1].rearrange("p t m s -> p (t m s)"),
             )
 
-        def collect(copy, s):
-            for h in range(2):
-                copy(z_half[h][:, s, :], z[s][:, h * HALF : (h + 1) * HALF])
+        def move(plane):
+            for s in range(2):
+                nc.sync.dma_start(z_all[64 * plane : 64 * plane + 64, s, :], z[plane][64 * s : 64 * s + 64, 0:S])
 
         gather(0)
         scatter(0)
-        collect(nc.sync.dma_start, 0)
+        move(0)
         gather(1)
         gather(2)
         scatter(1)
-        collect(nc.sync.dma_start, 1)
+        move(1)
         gather(3)
         scatter(2)
-        collect(on_scalar, 2)
+        on_scalar(z_all[:, 2, :], z[2][:, 0:S])
         scatter(3)
         quant_w2(0, 2)
         quant_w2(2, 4)
-        on_scalar(z_half[0][:, 3, 0:CHUNK], z[3][:, 0:CHUNK])
-        on_scalar(z_half[0][:, 3, CHUNK:HALF], z[3][:, CHUNK:HALF])
-        on_scalar(z_half[1][:, 3, :], z[3][:, HALF:S])
+        on_scalar(z_all[:, 3, 0:CHUNK], z[3][:, 0:CHUNK])
+        on_scalar(z_all[:, 3, CHUNK:HALF], z[3][:, CHUNK:HALF])
+        on_scalar(z_all[:, 3, HALF:S], z[3][:, HALF:S])
 
         z_g = [keep.tile([P, CHUNK * PACK], BF16, name=f"z_g{c}", align_bytes=64) for c in range(4)]
         z_c = [keep.tile([P, HALF], U32, name=f"z_c{h}", align_bytes=64) for h in range(2)]
@@ -189,13 +203,13 @@ def tile_picked_ycutmix_relu_po_kernel(
             cols = slice(h * HALF, (h + 1) * HALF)
             nc.sync.dma_start(out_words[:, cols], y_c[:, cols].bitcast(I32))
 
-        weave(on_vector, z_g[0][:], z_half[0][:], 0, CHUNK)
-        weave(on_vector, z_g[1][:], z_half[0][:], CHUNK, CHUNK + Z_SPLIT)
-        weave(on_scalar, z_g[1][:, Z_SPLIT * PACK :], z_half[0][:], CHUNK + Z_SPLIT, HALF)
+        weave(on_vector, z_g[0][:], z_all[:], 0, CHUNK)
+        weave(on_vector, z_g[1][:], z_all[:], CHUNK, CHUNK + Z_SPLIT)
+        weave(on_scalar, z_g[1][:, Z_SPLIT * PACK :], z_all[:], CHUNK + Z_SPLIT, HALF)
         quant_z(0)
         quant_z(1)
-        weave(on_scalar, z_g[2][:], z_half[1][:], 0, CHUNK)
-        weave(on_vector, z_g[3][:], z_half[1][:], CHUNK, HALF)
+        weave(on_scalar, z_g[2][:], z_all[:], HALF, HALF + CHUNK)
+        weave(on_vector, z_g[3][:], z_all[:], HALF + CHUNK, S)
         quant_z(2)
         quant_z(3)
         layer2(0, 0, 0, CHUNK, banks[0])

@@ -103,31 +103,16 @@ def tile_picked_ycutmix_relu_po_kernel(
             pick_words(first, last)
         cast_w1(on_vector, 1, 0)
         cast_w1(on_vector, 1, 1)
-        for s in range(1, PACK):
-            quant_w1(s)
+        quant_w1(1)
+        quant_w1(2)
         for c, (first, last) in enumerate(pieces):
             layer1(0, first, last, banks[c])
-        for h in range(2):
-            layer1(1, h * HALF, (h + 1) * HALF, banks[3 + h])
-        layer1(2, 0, S, banks[5])
-        layer1(3, 0, S, banks[6])
-
-        w2_g = keep.tile([P, PACK, P, PACK], BF16, name="w2_g", align_bytes=64)
-        w2_c = keep.tile([P, N], U32, name="w2_c", align_bytes=64)
-        w2_s = keep.tile([P, N], U8, name="w2_s", align_bytes=64)
-        for pair in range(2):
-            ts = slice(2 * pair, 2 * pair + 2)
-            for piece in range(2):
-                ms = slice(64 * piece, 64 * piece + 64)
-                nc.scalar.activation(
-                    w2_g[:].rearrange("p t m s -> p m s t")[:, ms, :, ts],
-                    w2_raw[:].rearrange("p s (m t) -> p m s t", t=PACK)[:, ms, :, ts],
-                    IDENTITY,
-                    bias=z[2 + piece][:, S : S + 1] if pair == 0 else 0.0,
-                )
+        for s in (1, 2):
+            for h in range(2):
+                layer1(s, h * HALF, (h + 1) * HALF, banks[1 + 2 * s + h])
 
         picked = [
-            keep.tile([P, V], F32, name=f"picked{s}", tag="w1_g1" if s == 0 else f"picked{s}", align_bytes=64)
+            keep.tile([P, V], F32, name=f"picked{s}", tag="w1_g0" if s == 0 else f"picked{s}", align_bytes=64)
             for s in range(PACK)
         ]
 
@@ -148,6 +133,23 @@ def tile_picked_ycutmix_relu_po_kernel(
                 nc.sync.dma_start(z_all[64 * plane : 64 * plane + 64, s, :], z[plane][64 * s : 64 * s + 64, 0:S])
 
         gather(0)
+        quant_w1(3)
+        layer1(3, 0, S, banks[7])
+
+        w2_g = keep.tile([P, PACK, P, PACK], BF16, name="w2_g", align_bytes=64)
+        w2_c = keep.tile([P, N], U32, name="w2_c", align_bytes=64)
+        w2_s = keep.tile([P, N], U8, name="w2_s", align_bytes=64)
+        for pair in range(2):
+            ts = slice(2 * pair, 2 * pair + 2)
+            for piece in range(2):
+                ms = slice(64 * piece, 64 * piece + 64)
+                nc.scalar.activation(
+                    w2_g[:].rearrange("p t m s -> p m s t")[:, ms, :, ts],
+                    w2_raw[:].rearrange("p s (m t) -> p m s t", t=PACK)[:, ms, :, ts],
+                    IDENTITY,
+                    bias=z[2 + piece][:, S : S + 1] if pair == 0 else 0.0,
+                )
+
         scatter(0)
         move(0)
         gather(1)

@@ -44,7 +44,7 @@ def tile_picked_ycutmix_relu_po_kernel(
         xs = keep.tile([P, T], U8, name="xs", align_bytes=64)
         w1_raw = [keep.tile([P, PACK, HALF], F32, name=f"w1_raw{h}", align_bytes=64) for h in range(2)]
         w2_raw = keep.tile([P, PACK, N], F32, name="w2_raw", align_bytes=64)
-        z_all = keep.tile([P, PACK, S], F32, name="z_all", align_bytes=64)
+        z_all = [keep.tile([P, PACK, HALF], F32, name=f"z_all{h}", tag=f"z_all{h}", align_bytes=64) for h in range(2)]
 
         nc.vector.memset(xs[:].bitcast(I32), 0)
         w1_rows = w1.rearrange("(p j) c -> p j c", j=PACK)
@@ -129,8 +129,11 @@ def tile_picked_ycutmix_relu_po_kernel(
             )
 
         def move(plane):
-            for s in range(2):
-                nc.sync.dma_start(z_all[64 * plane : 64 * plane + 64, s, :], z[plane][64 * s : 64 * s + 64, 0:S])
+            for h in range(2):
+                for s in range(2):
+                    nc.sync.dma_start(
+                        z_all[h][64 * plane : 64 * plane + 64, s, :], z[plane][64 * s : 64 * s + 64, h * HALF : (h + 1) * HALF]
+                    )
 
         gather(0)
         quant_w1(3)
@@ -158,18 +161,19 @@ def tile_picked_ycutmix_relu_po_kernel(
         move(1)
         gather(3)
         scatter(2)
-        on_scalar(z_all[:, 2, :], z[2][:, 0:S])
+        for h in range(2):
+            on_scalar(z_all[h][:, 2, :], z[2][:, h * HALF : (h + 1) * HALF])
         scatter(3)
         quant_w2(0, 2)
         quant_w2(2, 4)
-        on_scalar(z_all[:, 3, 0:CHUNK], z[3][:, 0:CHUNK])
-        on_scalar(z_all[:, 3, CHUNK:HALF], z[3][:, CHUNK:HALF])
-        on_scalar(z_all[:, 3, HALF:S], z[3][:, HALF:S])
+        on_scalar(z_all[0][:, 3, 0:CHUNK], z[3][:, 0:CHUNK])
+        on_scalar(z_all[0][:, 3, CHUNK:HALF], z[3][:, CHUNK:HALF])
+        on_scalar(z_all[1][:, 3, :], z[3][:, HALF:S])
 
         z_g = [keep.tile([P, CHUNK * PACK], BF16, name=f"z_g{c}", align_bytes=64) for c in range(4)]
         z_c = [keep.tile([P, HALF], U32, name=f"z_c{h}", align_bytes=64) for h in range(2)]
         z_s = [keep.tile([P, HALF], U8, name=f"z_s{h}", align_bytes=64) for h in range(2)]
-        y = [keep.tile([P, PACK, HALF], F32, name=f"y{h}", align_bytes=64) for h in range(2)]
+        y = [keep.tile([P, PACK, HALF], F32, name=f"y{h}", tag=("z_all1", "y1")[h], align_bytes=64) for h in range(2)]
         y_g = [keep.tile([P, CHUNK * PACK], BF16, name=f"y_g{c}", align_bytes=64) for c in range(4)]
         y_c = keep.tile([P, S], U32, name="y_c", align_bytes=64)
         y_s = keep.tile([P, S], U8, name="y_s", align_bytes=64)
@@ -205,13 +209,13 @@ def tile_picked_ycutmix_relu_po_kernel(
             cols = slice(h * HALF, (h + 1) * HALF)
             nc.sync.dma_start(out_words[:, cols], y_c[:, cols].bitcast(I32))
 
-        weave(on_vector, z_g[0][:], z_all[:], 0, CHUNK)
-        weave(on_vector, z_g[1][:], z_all[:], CHUNK, CHUNK + Z_SPLIT)
-        weave(on_scalar, z_g[1][:, Z_SPLIT * PACK :], z_all[:], CHUNK + Z_SPLIT, HALF)
+        weave(on_vector, z_g[0][:], z_all[0][:], 0, CHUNK)
+        weave(on_vector, z_g[1][:], z_all[0][:], CHUNK, CHUNK + Z_SPLIT)
+        weave(on_scalar, z_g[1][:, Z_SPLIT * PACK :], z_all[0][:], CHUNK + Z_SPLIT, HALF)
         quant_z(0)
         quant_z(1)
-        weave(on_scalar, z_g[2][:], z_all[:], HALF, HALF + CHUNK)
-        weave(on_vector, z_g[3][:], z_all[:], HALF + CHUNK, S)
+        weave(on_scalar, z_g[2][:], z_all[1][:], 0, CHUNK)
+        weave(on_vector, z_g[3][:], z_all[1][:], CHUNK, HALF)
         quant_z(2)
         quant_z(3)
         layer2(0, 0, 0, CHUNK, banks[0])

@@ -10,7 +10,7 @@ U16 = mybir.dt.uint16
 U8 = mybir.dt.uint8
 FP8X4 = mybir.dt.float8_e4m3fn_x4
 RELU = mybir.ActivationFunctionType.Relu
-IDENTITY = mybir.ActivationFunctionType.Identity
+COPY = mybir.ActivationFunctionType.Copy
 
 P = 128
 PACK = 4
@@ -67,9 +67,8 @@ def tile_picked_ycutmix_relu_po_kernel(
         w1_c = [keep.tile([P, P], U32, name=f"w1_c{s}", align_bytes=64) for s in range(PACK)]
         w1_s = [keep.tile([P, P], U8, name=f"w1_s{s}", align_bytes=64) for s in range(PACK)]
         banks = [psum.tile([P, 512], F32, name=f"bank{b}") for b in range(8)]
-        z = [keep.tile([P, S + (SPARE if s >= 1 else 0)], F32, name=f"z{s}", align_bytes=64) for s in range(PACK)]
-        for s in (1, 2):
-            nc.gpsimd.memset(z[s][:, S : S + SPARE], 0.0)
+        z = [keep.tile([P, S + (SPARE if s >= 2 else 0)], F32, name=f"z{s}", align_bytes=64) for s in range(PACK)]
+        nc.gpsimd.memset(z[2][:, S : S + SPARE], 0.0)
         nc.scalar.copy(z[3][:, S : S + SPARE], z[2][:, S : S + SPARE])
         on_vector, on_scalar = nc.vector.tensor_copy, nc.scalar.copy
 
@@ -92,8 +91,7 @@ def tile_picked_ycutmix_relu_po_kernel(
                 out=bank[:, 0 : last - first], lhsT=w1_c[s][:].bitcast(FP8X4), lhsT_scale=w1_s[s][:],
                 rhs=xq_w[:, first:last].bitcast(FP8X4), rhs_scale=xq_s[:, first:last], start=True, stop=True,
             )
-            zero = z[s - 1][:, S : S + 1] if s >= 2 else 0.0
-            nc.scalar.activation(z[s][:, first:last], bank[:, 0 : last - first], RELU, bias=zero)
+            nc.scalar.activation(z[s][:, first:last], bank[:, 0 : last - first], RELU)
 
         cast_w1(on_scalar, 0, 0)
         cast_w1(on_scalar, 0, 1)
@@ -107,9 +105,8 @@ def tile_picked_ycutmix_relu_po_kernel(
         quant_w1(2)
         for c, (first, last) in enumerate(pieces):
             layer1(0, first, last, banks[c])
-        for s in (1, 2):
-            for h in range(2):
-                layer1(s, h * HALF, (h + 1) * HALF, banks[1 + 2 * s + h])
+        for h in range(2):
+            layer1(1, h * HALF, (h + 1) * HALF, banks[3 + h])
 
         picked = [
             keep.tile([P, V], F32, name=f"picked{s}", tag="w1_g0" if s == 0 else f"picked{s}", align_bytes=64)
@@ -117,10 +114,16 @@ def tile_picked_ycutmix_relu_po_kernel(
         ]
 
         def gather(s):
-            nc.vector.tensor_copy(picked[s][:], z[s][:].indirect(give_t[:]))
+            if s == 0:
+                nc.vector.tensor_copy(picked[s][:], z[s][:].indirect(give_t[:]))
+            else:
+                nc.scalar.activation(picked[s][:], z[s][:].indirect(give_t[:]), COPY)
 
         def scatter(s):
-            nc.vector.tensor_copy(z[s][:].indirect(take_t[:]), picked[s][:])
+            if s < 2:
+                nc.vector.tensor_copy(z[s][:].indirect(take_t[:]), picked[s][:])
+            else:
+                nc.scalar.activation(z[s][:].indirect(take_t[:]), picked[s][:], COPY)
 
         def quant_w2(t0, t1):
             nc.vector.quantize_mx(
@@ -135,37 +138,41 @@ def tile_picked_ycutmix_relu_po_kernel(
                         z_all[h][64 * plane : 64 * plane + 64, s, :], z[plane][64 * s : 64 * s + 64, h * HALF : (h + 1) * HALF]
                     )
 
-        gather(0)
-        quant_w1(3)
-        layer1(3, 0, S, banks[7])
-
         w2_g = keep.tile([P, PACK, P, PACK], BF16, name="w2_g", align_bytes=64)
         w2_c = keep.tile([P, N], U32, name="w2_c", align_bytes=64)
         w2_s = keep.tile([P, N], U8, name="w2_s", align_bytes=64)
-        for pair in range(2):
-            ts = slice(2 * pair, 2 * pair + 2)
-            for piece in range(2):
-                ms = slice(64 * piece, 64 * piece + 64)
-                nc.scalar.activation(
-                    w2_g[:].rearrange("p t m s -> p m s t")[:, ms, :, ts],
-                    w2_raw[:].rearrange("p s (m t) -> p m s t", t=PACK)[:, ms, :, ts],
-                    IDENTITY,
-                    bias=z[2 + piece][:, S : S + 1] if pair == 0 else 0.0,
-                )
 
+        def cast_w2(pair, first, last, zero=None):
+            ts = slice(2 * pair, 2 * pair + 2)
+            ms = slice(first, last)
+            dst = w2_g[:].rearrange("p t m s -> p m s t")[:, ms, :, ts]
+            src = w2_raw[:].rearrange("p s (m t) -> p m s t", t=PACK)[:, ms, :, ts]
+            if zero is None:
+                on_vector(dst, src)
+            else:
+                nc.vector.tensor_scalar_add(dst, src, zero)
+
+        gather(0)
+        quant_w1(3)
+        gather(1)
+        for h in range(2):
+            layer1(2, h * HALF, (h + 1) * HALF, banks[5 + h])
         scatter(0)
         move(0)
-        gather(1)
-        gather(2)
         scatter(1)
         move(1)
+        layer1(3, 0, S, banks[7])
+        gather(2)
         gather(3)
+        cast_w2(0, 0, 32, z[2][:, S : S + 1])
+        cast_w2(0, 32, P, z[3][:, S : S + 1])
         scatter(2)
-        for h in range(2):
-            on_scalar(z_all[h][:, 2, :], z[2][:, h * HALF : (h + 1) * HALF])
         scatter(3)
+        cast_w2(1, 0, P)
         quant_w2(0, 2)
+        on_vector(z_all[0][:, 2, :], z[2][:, 0:HALF])
         quant_w2(2, 4)
+        on_vector(z_all[1][:, 2, :], z[2][:, HALF:S])
         on_scalar(z_all[0][:, 3, 0:CHUNK], z[3][:, 0:CHUNK])
         on_scalar(z_all[0][:, 3, CHUNK:HALF], z[3][:, CHUNK:HALF])
         on_scalar(z_all[1][:, 3, :], z[3][:, HALF:S])

@@ -10,6 +10,7 @@ U16 = mybir.dt.uint16
 U8 = mybir.dt.uint8
 FP8X4 = mybir.dt.float8_e4m3fn_x4
 RELU = mybir.ActivationFunctionType.Relu
+ADD = mybir.AluOpType.add
 COPY = mybir.ActivationFunctionType.Copy
 
 P = 128
@@ -142,15 +143,8 @@ def tile_picked_ycutmix_relu_po_kernel(
         w2_c = keep.tile([P, N], U32, name="w2_c", align_bytes=64)
         w2_s = keep.tile([P, N], U8, name="w2_s", align_bytes=64)
 
-        def cast_w2(pair, first, last, zero=None):
-            ts = slice(2 * pair, 2 * pair + 2)
-            ms = slice(first, last)
-            dst = w2_g[:].rearrange("p t m s -> p m s t")[:, ms, :, ts]
-            src = w2_raw[:].rearrange("p s (m t) -> p m s t", t=PACK)[:, ms, :, ts]
-            if zero is None:
-                on_vector(dst, src)
-            else:
-                nc.vector.tensor_scalar_add(dst, src, zero)
+        w2_dst = w2_g[:].rearrange("p t m s -> p m s t")
+        w2_src = w2_raw[:].rearrange("p s (m t) -> p m s t", t=PACK)
 
         gather(0)
         quant_w1(3)
@@ -164,18 +158,16 @@ def tile_picked_ycutmix_relu_po_kernel(
         layer1(3, 0, S, banks[7])
         gather(2)
         gather(3)
-        cast_w2(0, 0, 32, z[2][:, S : S + 1])
-        cast_w2(0, 32, P, z[3][:, S : S + 1])
+        nc.vector.tensor_scalar(w2_dst[:, 0:SPARE], w2_src[:, 0:SPARE], z[2][:, S : S + 1], z[3][:, S : S + 1], ADD, ADD)
         scatter(2)
         scatter(3)
-        cast_w2(1, 0, P)
-        quant_w2(0, 2)
+        on_vector(w2_dst[:, SPARE:P], w2_src[:, SPARE:P])
         on_vector(z_all[0][:, 2, :], z[2][:, 0:HALF])
-        quant_w2(2, 4)
+        quant_w2(0, 4)
         on_vector(z_all[1][:, 2, :], z[2][:, HALF:S])
         on_scalar(z_all[0][:, 3, 0:CHUNK], z[3][:, 0:CHUNK])
         on_scalar(z_all[0][:, 3, CHUNK:HALF], z[3][:, CHUNK:HALF])
-        on_scalar(z_all[1][:, 3, :], z[3][:, HALF:S])
+        on_vector(z_all[1][:, 3, :], z[3][:, HALF:S])
 
         z_g = [keep.tile([P, CHUNK * PACK], BF16, name=f"z_g{c}", align_bytes=64) for c in range(4)]
         z_c = [keep.tile([P, HALF], U32, name=f"z_c{h}", align_bytes=64) for h in range(2)]

@@ -11,6 +11,7 @@ U8 = mybir.dt.uint8
 FP8X4 = mybir.dt.float8_e4m3fn_x4
 RELU = mybir.ActivationFunctionType.Relu
 ADD = mybir.AluOpType.add
+MULT = mybir.AluOpType.mult
 COPY = mybir.ActivationFunctionType.Copy
 
 P = 128
@@ -126,10 +127,10 @@ def tile_picked_ycutmix_relu_po_kernel(
             else:
                 nc.scalar.activation(z[s][:].indirect(take_t[:]), picked[s][:], COPY)
 
-        def quant_w2(t0, t1):
+        def quant_w2(t0, t1, rounded):
             nc.vector.quantize_mx(
                 out=w2_c[:, t0 * P : t1 * P].bitcast(FP8X4), scales=w2_s[:, t0 * P : t1 * P],
-                in_=w2_g[:, t0:t1].rearrange("p t m s -> p (t m s)"),
+                in_=rounded,
             )
 
         def move(plane):
@@ -139,15 +140,18 @@ def tile_picked_ycutmix_relu_po_kernel(
                         z_all[h][64 * plane : 64 * plane + 64, s, :], z[plane][64 * s : 64 * s + 64, h * HALF : (h + 1) * HALF]
                     )
 
-        w2_g = keep.tile([P, PACK, P, PACK], BF16, name="w2_g", align_bytes=64)
+        w2_g = keep.tile([P, PACK - 1, P, PACK], BF16, name="w2_g", align_bytes=64)
         w2_c = keep.tile([P, N], U32, name="w2_c", align_bytes=64)
         w2_s = keep.tile([P, N], U8, name="w2_s", align_bytes=64)
 
         w2_dst = w2_g[:].rearrange("p t m s -> p m s t")
-        w2_src = w2_raw[:].rearrange("p s (m t) -> p m s t", t=PACK)
+        w2_all = w2_raw[:].rearrange("p s (m t) -> p m s t", t=PACK)
+        w2_src = w2_all[:, :, :, 0 : PACK - 1]
 
         gather(0)
         quant_w1(3)
+        w2_last = keep.tile([P, P, PACK], BF16, name="w2_last", tag="w1_g1", align_bytes=64)
+        nc.gpsimd.tensor_scalar(w2_last[:], w2_all[:, :, :, PACK - 1], 1.0, 0.0, MULT, ADD)
         gather(1)
         for h in range(2):
             layer1(2, h * HALF, (h + 1) * HALF, banks[5 + h])
@@ -163,7 +167,8 @@ def tile_picked_ycutmix_relu_po_kernel(
         scatter(3)
         on_vector(w2_dst[:, SPARE:P], w2_src[:, SPARE:P])
         on_vector(z_all[0][:, 2, :], z[2][:, 0:HALF])
-        quant_w2(0, 4)
+        quant_w2(0, 3, w2_g[:].rearrange("p t m s -> p (t m s)"))
+        quant_w2(3, 4, w2_last[:].rearrange("p m s -> p (m s)"))
         on_vector(z_all[1][:, 2, :], z[2][:, HALF:S])
         on_scalar(z_all[0][:, 3, 0:CHUNK], z[3][:, 0:CHUNK])
         on_scalar(z_all[0][:, 3, CHUNK:HALF], z[3][:, CHUNK:HALF])

@@ -69,9 +69,10 @@ def tile_picked_ycutmix_relu_po_kernel(
         w1_c = [keep.tile([P, P], U32, name=f"w1_c{s}", align_bytes=64) for s in range(PACK)]
         w1_s = [keep.tile([P, P], U8, name=f"w1_s{s}", align_bytes=64) for s in range(PACK)]
         banks = [psum.tile([P, 512], F32, name=f"bank{b}") for b in range(8)]
-        z = [keep.tile([P, S + (SPARE if s >= 2 else 0)], F32, name=f"z{s}", align_bytes=64) for s in range(PACK)]
-        nc.gpsimd.memset(z[2][:, S : S + SPARE], 0.0)
-        nc.scalar.copy(z[3][:, S : S + SPARE], z[2][:, S : S + SPARE])
+        z = [keep.tile([P, S + (SPARE if s == 3 else 0)], F32, name=f"z{s}", align_bytes=64) for s in range(PACK)]
+        zeros = keep.tile([P, SPARE], F32, name="zeros", align_bytes=64)
+        nc.gpsimd.memset(zeros[:], 0.0)
+        nc.scalar.copy(z[3][:, S : S + SPARE], zeros[:])
         on_vector, on_scalar = nc.vector.tensor_copy, nc.scalar.copy
 
         def cast_w1(copy, h, pair):
@@ -122,7 +123,7 @@ def tile_picked_ycutmix_relu_po_kernel(
                 nc.scalar.activation(picked[s][:], z[s][:].indirect(give_t[:]), COPY)
 
         def scatter(s):
-            if s < 2:
+            if s != 2:
                 nc.vector.tensor_copy(z[s][:].indirect(take_t[:]), picked[s][:])
             else:
                 nc.scalar.activation(z[s][:].indirect(take_t[:]), picked[s][:], COPY)
@@ -140,18 +141,19 @@ def tile_picked_ycutmix_relu_po_kernel(
                         z_all[h][64 * plane : 64 * plane + 64, s, :], z[plane][64 * s : 64 * s + 64, h * HALF : (h + 1) * HALF]
                     )
 
-        w2_g = keep.tile([P, PACK - 1, P, PACK], BF16, name="w2_g", align_bytes=64)
+        w2_g = keep.tile([P, 2, P, PACK], BF16, name="w2_g", align_bytes=64)
         w2_c = keep.tile([P, N], U32, name="w2_c", align_bytes=64)
         w2_s = keep.tile([P, N], U8, name="w2_s", align_bytes=64)
 
         w2_dst = w2_g[:].rearrange("p t m s -> p m s t")
         w2_all = w2_raw[:].rearrange("p s (m t) -> p m s t", t=PACK)
-        w2_src = w2_all[:, :, :, 0 : PACK - 1]
+        w2_src = w2_all[:, :, :, 0:2]
 
         gather(0)
         quant_w1(3)
-        w2_last = keep.tile([P, P, PACK], BF16, name="w2_last", tag="w1_g1", align_bytes=64)
-        nc.gpsimd.tensor_scalar(w2_last[:], w2_all[:, :, :, PACK - 1], 1.0, 0.0, MULT, ADD)
+        w2_last = keep.tile([P, 2, P, PACK], BF16, name="w2_last", tag="w1_g1", align_bytes=64)
+        for t in (2, 3):
+            nc.gpsimd.tensor_scalar(w2_last[:, t - 2], w2_all[:, :, :, t], 1.0, 0.0, MULT, ADD)
         gather(1)
         for h in range(2):
             layer1(2, h * HALF, (h + 1) * HALF, banks[5 + h])
@@ -162,16 +164,16 @@ def tile_picked_ycutmix_relu_po_kernel(
         layer1(3, 0, S, banks[7])
         gather(2)
         gather(3)
-        nc.vector.tensor_scalar(w2_dst[:, 0:SPARE], w2_src[:, 0:SPARE], z[2][:, S : S + 1], z[3][:, S : S + 1], ADD, ADD)
         scatter(2)
-        scatter(3)
+        nc.vector.tensor_scalar_add(w2_dst[:, 0:SPARE], w2_src[:, 0:SPARE], z[3][:, S : S + 1])
         on_vector(w2_dst[:, SPARE:P], w2_src[:, SPARE:P])
-        on_vector(z_all[0][:, 2, :], z[2][:, 0:HALF])
-        quant_w2(0, 3, w2_g[:].rearrange("p t m s -> p (t m s)"))
-        quant_w2(3, 4, w2_last[:].rearrange("p m s -> p (m s)"))
-        on_vector(z_all[1][:, 2, :], z[2][:, HALF:S])
+        scatter(3)
+        quant_w2(0, 2, w2_g[:].rearrange("p t m s -> p (t m s)"))
+        quant_w2(2, 4, w2_last[:].rearrange("p t m s -> p (t m s)"))
+        on_scalar(z_all[0][:, 2, :], z[2][:, 0:HALF])
         on_scalar(z_all[0][:, 3, 0:CHUNK], z[3][:, 0:CHUNK])
         on_scalar(z_all[0][:, 3, CHUNK:HALF], z[3][:, CHUNK:HALF])
+        on_scalar(z_all[1][:, 2, :], z[2][:, HALF:S])
         on_vector(z_all[1][:, 3, :], z[3][:, HALF:S])
 
         z_g = [keep.tile([P, CHUNK * PACK], BF16, name=f"z_g{c}", align_bytes=64) for c in range(4)]

@@ -10,9 +10,9 @@ U16 = mybir.dt.uint16
 U8 = mybir.dt.uint8
 FP8X4 = mybir.dt.float8_e4m3fn_x4
 RELU = mybir.ActivationFunctionType.Relu
+COPY = mybir.ActivationFunctionType.Copy
 ADD = mybir.AluOpType.add
 MULT = mybir.AluOpType.mult
-COPY = mybir.ActivationFunctionType.Copy
 
 P = 128
 PACK = 4
@@ -21,9 +21,14 @@ S = 512
 H = 512
 N = 512
 V = 128
+ENTRIES = 16
+QUADRANTS = 4
+BANKS = 8
 HALF = 256
 CHUNK = 128
+SIDE = 64
 SPARE = 8
+W2_HEAD = 8
 Z_SPLIT = 64
 Y_SPLIT = 56
 FLOPS = 2 * 2 * 512 * 512 * 512
@@ -38,23 +43,25 @@ def tile_picked_ycutmix_relu_po_kernel(
         keep = ctx.enter_context(tc.tile_pool(name="keep", bufs=1))
         psum = ctx.enter_context(tc.psum_pool(name="psum", bufs=1))
 
-        offs_t = lists.tile([P, S // 16], U16, name="offs_t")
-        give_t = lists.tile([P, V // 16], U16, name="give_t")
-        take_t = lists.tile([P, V // 16], U16, name="take_t")
+        offs_t = lists.tile([P, S // ENTRIES], U16, name="offs_t")
+        give_t = lists.tile([P, V // ENTRIES], U16, name="give_t")
+        take_t = lists.tile([P, V // ENTRIES], U16, name="take_t")
 
         xw = keep.tile([P, T], I32, name="xw", align_bytes=64)
         xs = keep.tile([P, T], U8, name="xs", align_bytes=64)
-        w1_raw = [keep.tile([P, PACK, HALF], F32, name=f"w1_raw{h}", align_bytes=64) for h in range(2)]
+        w1_raw = [keep.tile([P, PACK, HALF], F32, name=f"w1_raw{half}", align_bytes=64) for half in range(2)]
         w2_raw = keep.tile([P, PACK, N], F32, name="w2_raw", align_bytes=64)
-        z_all = [keep.tile([P, PACK, HALF], F32, name=f"z_all{h}", tag=f"z_all{h}", align_bytes=64) for h in range(2)]
+        z_all = [
+            keep.tile([P, PACK, HALF], F32, name=f"z_all{half}", tag=f"z_all{half}", align_bytes=64) for half in range(2)
+        ]
 
         nc.vector.memset(xs[:].bitcast(I32), 0)
         w1_rows = w1.rearrange("(p j) c -> p j c", j=PACK)
         nc.sync.dma_start(offs_t[:], offs)
-        nc.sync.dma_start(w1_raw[0][:, 0:3], w1_rows[:, 0:3, 0:HALF])
-        for q in range(4):
+        nc.sync.dma_start(w1_raw[0][:, 0 : PACK - 1], w1_rows[:, 0 : PACK - 1, 0:HALF])
+        for q in range(QUADRANTS):
             nc.sync.dma_start(xs[32 * q : 32 * q + 4, :].bitcast(I32), x_scales[0, 4 * q : 4 * q + 4, :].bitcast(I32))
-        nc.sync.dma_start(w1_raw[0][:, 3], w1_rows[:, 3, 0:HALF])
+        nc.sync.dma_start(w1_raw[0][:, PACK - 1], w1_rows[:, PACK - 1, 0:HALF])
         nc.sync.dma_start(xw[:], x_words[0].rearrange("p n t -> p (n t)").bitcast(I32))
         nc.sync.dma_start(w1_raw[1][:], w1_rows[:, :, HALF:H])
         nc.sync.dma_start(give_t[:], give)
@@ -65,130 +72,141 @@ def tile_picked_ycutmix_relu_po_kernel(
         xq_s = keep.tile([P, S], U8, name="xq_s", align_bytes=64)
         nc.vector.tensor_copy(xq_s[:], xs[:].indirect(offs_t[:]))
 
-        w1_g = [keep.tile([P, 2, P, PACK], BF16, name=f"w1_g{pair}", tag=f"w1_g{pair}", align_bytes=64) for pair in range(2)]
-        w1_c = [keep.tile([P, P], U32, name=f"w1_c{s}", align_bytes=64) for s in range(PACK)]
-        w1_s = [keep.tile([P, P], U8, name=f"w1_s{s}", align_bytes=64) for s in range(PACK)]
-        banks = [psum.tile([P, 512], F32, name=f"bank{b}") for b in range(8)]
-        z = [keep.tile([P, S + (SPARE if s == 3 else 0)], F32, name=f"z{s}", align_bytes=64) for s in range(PACK)]
+        w1_g = [
+            keep.tile([P, 2, P, PACK], BF16, name=f"w1_g{pair}", tag=f"w1_g{pair}", align_bytes=64) for pair in range(2)
+        ]
+        w1_c = [keep.tile([P, P], U32, name=f"w1_c{plane}", align_bytes=64) for plane in range(PACK)]
+        w1_s = [keep.tile([P, P], U8, name=f"w1_s{plane}", align_bytes=64) for plane in range(PACK)]
+        banks = [psum.tile([P, 512], F32, name=f"bank{b}") for b in range(BANKS)]
+        z = [
+            keep.tile([P, S + (SPARE if plane == 3 else 0)], F32, name=f"z{plane}", align_bytes=64)
+            for plane in range(PACK)
+        ]
         zeros = keep.tile([P, SPARE], F32, name="zeros", align_bytes=64)
         nc.gpsimd.memset(zeros[:], 0.0)
         nc.scalar.copy(z[3][:, S : S + SPARE], zeros[:])
         on_vector, on_scalar = nc.vector.tensor_copy, nc.scalar.copy
 
-        def cast_w1(copy, h, pair):
-            src = w1_raw[h][:].rearrange("p j (m s) -> p m j s", s=PACK)[:, :, :, 2 * pair : 2 * pair + 2]
+        def round_w1(copy, half, pair):
+            src = w1_raw[half][:].rearrange("p j (m s) -> p m j s", s=PACK)[:, :, :, 2 * pair : 2 * pair + 2]
             if pair == 0:
-                dst = w1_g[0][:, h].rearrange("p (s m) j -> p m j s", s=2)
+                dst = w1_g[0][:, half].rearrange("p (s m) j -> p m j s", s=2)
             else:
-                dst = w1_g[1][:, :, 64 * h : 64 * h + 64].rearrange("p s m j -> p m j s")
+                dst = w1_g[1][:, :, SIDE * half : SIDE * (half + 1)].rearrange("p s m j -> p m j s")
             copy(dst, src)
 
         def pick_words(first, last):
-            nc.vector.tensor_copy(xq_w[:, first:last], xw[:].bitcast(U32).indirect(offs_t[:, first // 16 : last // 16]))
+            entries = offs_t[:, first // ENTRIES : last // ENTRIES]
+            nc.vector.tensor_copy(xq_w[:, first:last], xw[:].bitcast(U32).indirect(entries))
 
-        def quant_w1(s):
-            nc.vector.quantize_mx(out=w1_c[s][:].bitcast(FP8X4), scales=w1_s[s][:], in_=w1_g[s // 2][:, s % 2].rearrange("p m j -> p (m j)"))
+        def quant_w1(plane):
+            woven = w1_g[plane // 2][:, plane % 2].rearrange("p m j -> p (m j)")
+            nc.vector.quantize_mx(out=w1_c[plane][:].bitcast(FP8X4), scales=w1_s[plane][:], in_=woven)
 
-        def layer1(s, first, last, bank):
+        def layer1(plane, first, last, bank):
             nc.tensor.matmul_mx(
-                out=bank[:, 0 : last - first], lhsT=w1_c[s][:].bitcast(FP8X4), lhsT_scale=w1_s[s][:],
+                out=bank[:, 0 : last - first], lhsT=w1_c[plane][:].bitcast(FP8X4), lhsT_scale=w1_s[plane][:],
                 rhs=xq_w[:, first:last].bitcast(FP8X4), rhs_scale=xq_s[:, first:last], start=True, stop=True,
             )
-            nc.scalar.activation(z[s][:, first:last], bank[:, 0 : last - first], RELU)
+            nc.scalar.activation(z[plane][:, first:last], bank[:, 0 : last - first], RELU)
 
-        cast_w1(on_scalar, 0, 0)
-        cast_w1(on_scalar, 0, 1)
+        round_w1(on_scalar, 0, 0)
+        round_w1(on_scalar, 0, 1)
         quant_w1(0)
         pieces = ((0, HALF), (HALF, HALF + CHUNK), (HALF + CHUNK, S))
         for first, last in pieces:
             pick_words(first, last)
-        cast_w1(on_vector, 1, 0)
-        cast_w1(on_vector, 1, 1)
+        round_w1(on_vector, 1, 0)
+        round_w1(on_vector, 1, 1)
         quant_w1(1)
         quant_w1(2)
-        for c, (first, last) in enumerate(pieces):
-            layer1(0, first, last, banks[c])
-        for h in range(2):
-            layer1(1, h * HALF, (h + 1) * HALF, banks[3 + h])
+        for b, (first, last) in enumerate(pieces):
+            layer1(0, first, last, banks[b])
+        for half in range(2):
+            layer1(1, half * HALF, (half + 1) * HALF, banks[3 + half])
 
         picked = [
-            keep.tile([P, V], F32, name=f"picked{s}", tag="w1_g0" if s == 0 else f"picked{s}", align_bytes=64)
-            for s in range(PACK)
+            keep.tile(
+                [P, V], F32, name=f"picked{plane}", tag="w1_g0" if plane == 0 else f"picked{plane}", align_bytes=64
+            )
+            for plane in range(PACK)
         ]
 
-        def gather(s):
-            if s == 0:
-                nc.vector.tensor_copy(picked[s][:], z[s][:].indirect(give_t[:]))
-            else:
-                nc.scalar.activation(picked[s][:], z[s][:].indirect(give_t[:]), COPY)
+        def on_scalar_indirect(dst, src):
+            nc.scalar.activation(dst, src, COPY)
 
-        def scatter(s):
-            if s != 2:
-                nc.vector.tensor_copy(z[s][:].indirect(take_t[:]), picked[s][:])
-            else:
-                nc.scalar.activation(z[s][:].indirect(take_t[:]), picked[s][:], COPY)
+        def gather(copy, plane):
+            copy(picked[plane][:], z[plane][:].indirect(give_t[:]))
 
-        def quant_w2(t0, t1, rounded):
-            nc.vector.quantize_mx(
-                out=w2_c[:, t0 * P : t1 * P].bitcast(FP8X4), scales=w2_s[:, t0 * P : t1 * P],
-                in_=rounded,
-            )
+        def scatter(copy, plane):
+            copy(z[plane][:].indirect(take_t[:]), picked[plane][:])
 
         def move(plane):
-            for h in range(2):
+            for half in range(2):
                 for s in range(2):
                     nc.sync.dma_start(
-                        z_all[h][64 * plane : 64 * plane + 64, s, :], z[plane][64 * s : 64 * s + 64, h * HALF : (h + 1) * HALF]
+                        z_all[half][SIDE * plane : SIDE * (plane + 1), s, :],
+                        z[plane][SIDE * s : SIDE * (s + 1), half * HALF : (half + 1) * HALF],
                     )
 
-        w2_g = keep.tile([P, 2, P, PACK], BF16, name="w2_g", align_bytes=64)
+        w2_low = keep.tile([P, 2, P, PACK], BF16, name="w2_low", align_bytes=64)
         w2_c = keep.tile([P, N], U32, name="w2_c", align_bytes=64)
         w2_s = keep.tile([P, N], U8, name="w2_s", align_bytes=64)
+        w2_cols = w2_raw[:].rearrange("p s (m t) -> p m s t", t=PACK)
+        low_dst, low_src = w2_low[:].rearrange("p t m s -> p m s t"), w2_cols[:, :, :, 0:2]
 
-        w2_dst = w2_g[:].rearrange("p t m s -> p m s t")
-        w2_all = w2_raw[:].rearrange("p s (m t) -> p m s t", t=PACK)
-        w2_src = w2_all[:, :, :, 0:2]
+        def quant_w2(pair, woven):
+            cols = slice(pair * HALF, (pair + 1) * HALF)
+            nc.vector.quantize_mx(
+                out=w2_c[:, cols].bitcast(FP8X4), scales=w2_s[:, cols], in_=woven[:].rearrange("p t m s -> p (t m s)")
+            )
 
-        gather(0)
+        gather(on_vector, 0)
         quant_w1(3)
-        w2_last = keep.tile([P, 2, P, PACK], BF16, name="w2_last", tag="w1_g1", align_bytes=64)
-        for t in (2, 3):
-            nc.gpsimd.tensor_scalar(w2_last[:, t - 2], w2_all[:, :, :, t], 1.0, 0.0, MULT, ADD)
-        gather(1)
-        for h in range(2):
-            layer1(2, h * HALF, (h + 1) * HALF, banks[5 + h])
-        scatter(0)
+        w2_high = keep.tile([P, 2, P, PACK], BF16, name="w2_high", tag="w1_g1", align_bytes=64)
+        nc.gpsimd.tensor_scalar(
+            w2_high[:].rearrange("p t m s -> p m t s"), w2_cols[:, :, :, 2:4].rearrange("p m s t -> p m t s"),
+            1.0, 0.0, MULT, ADD,
+        )
+        gather(on_scalar_indirect, 1)
+        for half in range(2):
+            layer1(2, half * HALF, (half + 1) * HALF, banks[5 + half])
+        scatter(on_vector, 0)
         move(0)
-        scatter(1)
+        scatter(on_vector, 1)
         move(1)
         layer1(3, 0, S, banks[7])
-        gather(2)
-        gather(3)
-        scatter(2)
-        nc.vector.tensor_scalar_add(w2_dst[:, 0:SPARE], w2_src[:, 0:SPARE], z[3][:, S : S + 1])
-        on_vector(w2_dst[:, SPARE:P], w2_src[:, SPARE:P])
-        scatter(3)
-        quant_w2(0, 2, w2_g[:].rearrange("p t m s -> p (t m s)"))
-        quant_w2(2, 4, w2_last[:].rearrange("p t m s -> p (t m s)"))
+        gather(on_scalar_indirect, 2)
+        gather(on_scalar_indirect, 3)
+        scatter(on_scalar_indirect, 2)
+        nc.vector.tensor_scalar_add(low_dst[:, 0:W2_HEAD], low_src[:, 0:W2_HEAD], z[3][:, S : S + 1])
+        on_vector(low_dst[:, W2_HEAD:P], low_src[:, W2_HEAD:P])
+        scatter(on_vector, 3)
+        quant_w2(0, w2_low)
+        quant_w2(1, w2_high)
         on_scalar(z_all[0][:, 2, :], z[2][:, 0:HALF])
         on_scalar(z_all[0][:, 3, 0:CHUNK], z[3][:, 0:CHUNK])
         on_scalar(z_all[0][:, 3, CHUNK:HALF], z[3][:, CHUNK:HALF])
         on_scalar(z_all[1][:, 2, :], z[2][:, HALF:S])
         on_vector(z_all[1][:, 3, :], z[3][:, HALF:S])
 
-        z_g = [keep.tile([P, CHUNK * PACK], BF16, name=f"z_g{c}", align_bytes=64) for c in range(4)]
-        z_c = [keep.tile([P, HALF], U32, name=f"z_c{h}", align_bytes=64) for h in range(2)]
-        z_s = [keep.tile([P, HALF], U8, name=f"z_s{h}", align_bytes=64) for h in range(2)]
-        y = [keep.tile([P, PACK, HALF], F32, name=f"y{h}", tag=("z_all1", "y1")[h], align_bytes=64) for h in range(2)]
-        y_g = [keep.tile([P, CHUNK * PACK], BF16, name=f"y_g{c}", align_bytes=64) for c in range(4)]
+        chunks = S // CHUNK
+        z_g = [keep.tile([P, CHUNK * PACK], BF16, name=f"z_g{c}", align_bytes=64) for c in range(chunks)]
+        z_c = [keep.tile([P, HALF], U32, name=f"z_c{half}", align_bytes=64) for half in range(2)]
+        z_s = [keep.tile([P, HALF], U8, name=f"z_s{half}", align_bytes=64) for half in range(2)]
+        y = [
+            keep.tile([P, PACK, HALF], F32, name=f"y{half}", tag=("z_all1", "y1")[half], align_bytes=64)
+            for half in range(2)
+        ]
+        y_g = [keep.tile([P, CHUNK * PACK], BF16, name=f"y_g{c}", align_bytes=64) for c in range(chunks)]
         y_c = keep.tile([P, S], U32, name="y_c", align_bytes=64)
         y_s = keep.tile([P, S], U8, name="y_s", align_bytes=64)
         out_rows = out_0.rearrange("(p t) c -> p t c", t=PACK)
         out_words = out_1[0].rearrange("p n t -> p (n t)").bitcast(I32)
 
-        def weave(copy, grouped, rows, first, last):
+        def weave(copy, woven, rows, first, last):
             copy(
-                grouped[:, 0 : (last - first) * PACK].rearrange("p (a i s) -> p a s i", i=4, s=PACK),
+                woven[:, 0 : (last - first) * PACK].rearrange("p (a i s) -> p a s i", i=4, s=PACK),
                 rows[:, :, first:last].rearrange("p s (a i) -> p a s i", i=4),
             )
 
@@ -196,23 +214,23 @@ def tile_picked_ycutmix_relu_po_kernel(
             cols = slice((c % 2) * CHUNK, (c % 2 + 1) * CHUNK)
             nc.vector.quantize_mx(out=z_c[c // 2][:, cols].bitcast(FP8X4), scales=z_s[c // 2][:, cols], in_=z_g[c][:])
 
-        def layer2(h, t, first, last, bank, copy=on_scalar):
+        def layer2(half, t, first, last, bank, copy=on_scalar):
             nc.tensor.matmul_mx(
                 out=bank[:, 0 : last - first],
                 lhsT=w2_c[:, t * P : (t + 1) * P].bitcast(FP8X4), lhsT_scale=w2_s[:, t * P : (t + 1) * P],
-                rhs=z_c[h][:, first:last].bitcast(FP8X4), rhs_scale=z_s[h][:, first:last], start=True, stop=True,
+                rhs=z_c[half][:, first:last].bitcast(FP8X4), rhs_scale=z_s[half][:, first:last], start=True, stop=True,
             )
-            copy(y[h][:, t, first:last], bank[:, 0 : last - first])
+            copy(y[half][:, t, first:last], bank[:, 0 : last - first])
 
-        def store_y(h, t, count):
-            nc.sync.dma_start(out_rows[:, t : t + count, h * HALF : (h + 1) * HALF], y[h][:, t : t + count, :])
+        def store_y(half, t, count):
+            nc.sync.dma_start(out_rows[:, t : t + count, half * HALF : (half + 1) * HALF], y[half][:, t : t + count, :])
 
         def quant_y(c):
             cols = slice(c * CHUNK, (c + 1) * CHUNK)
             nc.vector.quantize_mx(out=y_c[:, cols].bitcast(FP8X4), scales=y_s[:, cols], in_=y_g[c][:])
 
-        def store_words(h):
-            cols = slice(h * HALF, (h + 1) * HALF)
+        def store_words(half):
+            cols = slice(half * HALF, (half + 1) * HALF)
             nc.sync.dma_start(out_words[:, cols], y_c[:, cols].bitcast(I32))
 
         weave(on_vector, z_g[0][:], z_all[0][:], 0, CHUNK)
@@ -224,6 +242,7 @@ def tile_picked_ycutmix_relu_po_kernel(
         weave(on_vector, z_g[3][:], z_all[1][:], CHUNK, HALF)
         quant_z(2)
         quant_z(3)
+
         layer2(0, 0, 0, CHUNK, banks[0])
         layer2(0, 0, CHUNK, HALF, banks[1])
         store_y(0, 0, 1)
@@ -237,6 +256,7 @@ def tile_picked_ycutmix_relu_po_kernel(
         weave(on_vector, y_g[1][:], y[0][:], CHUNK, HALF)
         quant_y(0)
         quant_y(1)
+
         for t in (0, 1):
             layer2(1, t, 0, HALF, banks[6 + t])
         store_y(1, 0, 2)
@@ -252,5 +272,5 @@ def tile_picked_ycutmix_relu_po_kernel(
         quant_y(2)
         quant_y(3)
         store_words(1)
-        for q in range(4):
+        for q in range(QUADRANTS):
             nc.scalar.dma_start(out_2[0, 4 * q : 4 * q + 4, :].bitcast(I32), y_s[32 * q : 32 * q + 4, :].bitcast(I32))

@@ -27,6 +27,7 @@ BANKS = 8
 HALF = 256
 CHUNK = 128
 SIDE = 64
+PAD = 16
 SPARE = 8
 W2_HEAD = 8
 Z_SPLIT = 64
@@ -49,10 +50,13 @@ def tile_picked_ycutmix_relu_po_kernel(
 
         xw = keep.tile([P, T], I32, name="xw", align_bytes=64)
         xs = keep.tile([P, T], U8, name="xs", align_bytes=64)
-        w1_raw = [keep.tile([P, PACK, HALF], F32, name=f"w1_raw{half}", align_bytes=64) for half in range(2)]
+        w1_raw = [
+            keep.tile([P, PACK, HALF + PAD], F32, name=f"w1_raw{half}", align_bytes=256)[:, :, 0:HALF] for half in range(2)
+        ]
         w2_raw = keep.tile([P, PACK, N], F32, name="w2_raw", align_bytes=64)
         z_all = [
-            keep.tile([P, PACK, HALF], F32, name=f"z_all{half}", tag=f"z_all{half}", align_bytes=64) for half in range(2)
+            keep.tile([P, PACK, HALF + PAD], F32, name=f"z_all{half}", tag=f"z_all{half}", align_bytes=256)[:, :, 0:HALF]
+            for half in range(2)
         ]
 
         nc.vector.memset(xs[:].bitcast(I32), 0)
@@ -195,7 +199,9 @@ def tile_picked_ycutmix_relu_po_kernel(
         z_c = [keep.tile([P, HALF], U32, name=f"z_c{half}", align_bytes=64) for half in range(2)]
         z_s = [keep.tile([P, HALF], U8, name=f"z_s{half}", align_bytes=64) for half in range(2)]
         y = [
-            keep.tile([P, PACK, HALF], F32, name=f"y{half}", tag=("z_all1", "y1")[half], align_bytes=64)
+            keep.tile([P, PACK, HALF + PAD], F32, name=f"y{half}", tag=("z_all1", "y1")[half], align_bytes=256)[
+                :, :, 0:HALF
+            ]
             for half in range(2)
         ]
         y_g = [keep.tile([P, CHUNK * PACK], BF16, name=f"y_g{c}", align_bytes=64) for c in range(chunks)]

@@ -212,8 +212,8 @@ def tile_picked_ycutmix_relu_po_kernel(
 
         def weave(copy, woven, rows, first, last):
             copy(
-                woven[:, 0 : (last - first) * PACK].rearrange("p (a i s) -> p a s i", i=4, s=PACK),
-                rows[:, :, first:last].rearrange("p s (a i) -> p a s i", i=4),
+                woven[:, 0 : (last - first) * PACK].rearrange("p (a i s) -> p a s i", i=2, s=PACK),
+                rows[:, :, first:last].rearrange("p s (a i) -> p a s i", i=2),
             )
 
         def quant_z(c):

@@ -192,14 +192,14 @@ def tile_picked_ycutmix_relu_po_kernel(
         on_scalar(z_all[0][:, 3, 0:CHUNK], z[3][:, 0:CHUNK])
         on_scalar(z_all[0][:, 3, CHUNK:HALF], z[3][:, CHUNK:HALF])
         on_scalar(z_all[1][:, 2, :], z[2][:, HALF:S])
-        on_vector(z_all[1][:, 3, :], z[3][:, HALF:S])
+        on_scalar(z_all[1][:, 3, :], z[3][:, HALF:S])
 
         chunks = S // CHUNK
         z_g = [keep.tile([P, CHUNK * PACK], BF16, name=f"z_g{c}", align_bytes=64) for c in range(chunks)]
         z_c = [keep.tile([P, HALF], U32, name=f"z_c{half}", align_bytes=64) for half in range(2)]
         z_s = [keep.tile([P, HALF], U8, name=f"z_s{half}", align_bytes=64) for half in range(2)]
         y = [
-            keep.tile([P, PACK, HALF + PAD], F32, name=f"y{half}", tag=("z_all1", "y1")[half], align_bytes=256)[
+            keep.tile([P, PACK, HALF + PAD], F32, name=f"y{half}", tag=("y0", "y1")[half], align_bytes=256)[
                 :, :, 0:HALF
             ]
             for half in range(2)
@@ -244,7 +244,7 @@ def tile_picked_ycutmix_relu_po_kernel(
         weave(on_scalar, z_g[1][:, Z_SPLIT * PACK :], z_all[0][:], CHUNK + Z_SPLIT, HALF)
         quant_z(0)
         quant_z(1)
-        weave(on_scalar, z_g[2][:], z_all[1][:], 0, CHUNK)
+        weave(on_vector, z_g[2][:], z_all[1][:], 0, CHUNK)
         weave(on_vector, z_g[3][:], z_all[1][:], CHUNK, HALF)
         quant_z(2)
         quant_z(3)

@@ -29,7 +29,6 @@ CHUNK = 128
 SIDE = 64
 PAD = 16
 SPARE = 8
-W2_HEAD = 8
 Z_SPLIT = 64
 Y_SPLIT = 56
 FLOPS = 2 * 2 * 512 * 512 * 512
@@ -99,10 +98,6 @@ def tile_picked_ycutmix_relu_po_kernel(
                 dst = w1_g[1][:, :, SIDE * half : SIDE * (half + 1)].rearrange("p s m j -> p m j s")
             copy(dst, src)
 
-        def pick_words(first, last):
-            entries = offs_t[:, first // ENTRIES : last // ENTRIES]
-            nc.vector.tensor_copy(xq_w[:, first:last], xw[:].bitcast(U32).indirect(entries))
-
         def quant_w1(plane):
             woven = w1_g[plane // 2][:, plane % 2].rearrange("p m j -> p (m j)")
             nc.vector.quantize_mx(out=w1_c[plane][:].bitcast(FP8X4), scales=w1_s[plane][:], in_=woven)
@@ -117,9 +112,10 @@ def tile_picked_ycutmix_relu_po_kernel(
         round_w1(on_scalar, 0, 0)
         round_w1(on_scalar, 0, 1)
         quant_w1(0)
-        pieces = ((0, HALF), (HALF, HALF + CHUNK), (HALF + CHUNK, S))
+        pieces = ((0, HALF), (HALF, S))
         for first, last in pieces:
-            pick_words(first, last)
+            entries = offs_t[:, first // ENTRIES : last // ENTRIES]
+            nc.vector.tensor_copy(xq_w[:, first:last], xw[:].bitcast(U32).indirect(entries))
         round_w1(on_vector, 1, 0)
         round_w1(on_vector, 1, 1)
         quant_w1(1)
@@ -153,23 +149,16 @@ def tile_picked_ycutmix_relu_po_kernel(
                         z[plane][SIDE * s : SIDE * (s + 1), half * HALF : (half + 1) * HALF],
                     )
 
-        w2_low = keep.tile([P, 2, P, PACK], BF16, name="w2_low", align_bytes=64)
         w2_c = keep.tile([P, N], U32, name="w2_c", align_bytes=64)
         w2_s = keep.tile([P, N], U8, name="w2_s", align_bytes=64)
         w2_cols = w2_raw[:].rearrange("p s (m t) -> p m s t", t=PACK)
-        low_dst, low_src = w2_low[:].rearrange("p t m s -> p m s t"), w2_cols[:, :, :, 0:2]
-
-        def quant_w2(pair, woven):
-            cols = slice(pair * HALF, (pair + 1) * HALF)
-            nc.vector.quantize_mx(
-                out=w2_c[:, cols].bitcast(FP8X4), scales=w2_s[:, cols], in_=woven[:].rearrange("p t m s -> p (t m s)")
-            )
 
         gather(on_vector, 0)
         quant_w1(3)
-        w2_high = keep.tile([P, 2, P, PACK], BF16, name="w2_high", tag="w1_g1", align_bytes=64)
+        w2_g = keep.tile([P, PACK, P, PACK], BF16, name="w2_g", tag="w1_g1", align_bytes=64)
+        low_dst, low_src = w2_g[:, 0:2].rearrange("p t m s -> p m s t"), w2_cols[:, :, :, 0:2]
         nc.gpsimd.tensor_scalar(
-            w2_high[:].rearrange("p t m s -> p m t s"), w2_cols[:, :, :, 2:4].rearrange("p m s t -> p m t s"),
+            w2_g[:, 2:4].rearrange("p t m s -> p m t s"), w2_cols[:, :, :, 2:4].rearrange("p m s t -> p m t s"),
             1.0, 0.0, MULT, ADD,
         )
         gather(on_scalar_indirect, 1)
@@ -183,19 +172,21 @@ def tile_picked_ycutmix_relu_po_kernel(
         gather(on_scalar_indirect, 2)
         gather(on_scalar_indirect, 3)
         scatter(on_scalar_indirect, 2)
-        nc.vector.tensor_scalar_add(low_dst[:, 0:W2_HEAD], low_src[:, 0:W2_HEAD], z[3][:, S : S + 1])
-        on_vector(low_dst[:, W2_HEAD:P], low_src[:, W2_HEAD:P])
+        nc.vector.tensor_scalar_add(low_dst, low_src, z[3][:, S : S + 1])
         scatter(on_vector, 3)
-        quant_w2(0, w2_low)
-        quant_w2(1, w2_high)
+        nc.vector.quantize_mx(
+            out=w2_c[:].bitcast(FP8X4), scales=w2_s[:], in_=w2_g[:].rearrange("p t m s -> p (t m s)")
+        )
         on_scalar(z_all[0][:, 2, :], z[2][:, 0:HALF])
-        on_scalar(z_all[0][:, 3, 0:CHUNK], z[3][:, 0:CHUNK])
-        on_scalar(z_all[0][:, 3, CHUNK:HALF], z[3][:, CHUNK:HALF])
+        on_scalar(z_all[0][:, 3, :], z[3][:, 0:HALF])
         on_scalar(z_all[1][:, 2, :], z[2][:, HALF:S])
         on_scalar(z_all[1][:, 3, :], z[3][:, HALF:S])
 
         chunks = S // CHUNK
-        z_g = [keep.tile([P, CHUNK * PACK], BF16, name=f"z_g{c}", align_bytes=64) for c in range(chunks)]
+        z_g = [
+            keep.tile([P, width * PACK], BF16, name=f"z_g{c}", align_bytes=64)
+            for c, width in enumerate((CHUNK, CHUNK, HALF))
+        ]
         z_c = [keep.tile([P, HALF], U32, name=f"z_c{half}", align_bytes=64) for half in range(2)]
         z_s = [keep.tile([P, HALF], U8, name=f"z_s{half}", align_bytes=64) for half in range(2)]
         y = [
@@ -216,17 +207,20 @@ def tile_picked_ycutmix_relu_po_kernel(
                 rows[:, :, first:last].rearrange("p s (a i) -> p a s i", i=2),
             )
 
-        def quant_z(c):
-            cols = slice((c % 2) * CHUNK, (c % 2 + 1) * CHUNK)
-            nc.vector.quantize_mx(out=z_c[c // 2][:, cols].bitcast(FP8X4), scales=z_s[c // 2][:, cols], in_=z_g[c][:])
+        def quant_z(woven, half, first, last):
+            cols = slice(first, last)
+            nc.vector.quantize_mx(out=z_c[half][:, cols].bitcast(FP8X4), scales=z_s[half][:, cols], in_=woven[:])
 
-        def layer2(half, t, first, last, bank, copy=on_scalar):
+        def product2(half, t, first, last, out):
             nc.tensor.matmul_mx(
-                out=bank[:, 0 : last - first],
+                out=out,
                 lhsT=w2_c[:, t * P : (t + 1) * P].bitcast(FP8X4), lhsT_scale=w2_s[:, t * P : (t + 1) * P],
                 rhs=z_c[half][:, first:last].bitcast(FP8X4), rhs_scale=z_s[half][:, first:last], start=True, stop=True,
             )
-            copy(y[half][:, t, first:last], bank[:, 0 : last - first])
+
+        def layer2(half, t, first, last, bank):
+            product2(half, t, first, last, bank[:, 0 : last - first])
+            on_scalar(y[half][:, t, first:last], bank[:, 0 : last - first])
 
         def store_y(half, t, count):
             nc.sync.dma_start(out_rows[:, t : t + count, half * HALF : (half + 1) * HALF], y[half][:, t : t + count, :])
@@ -242,12 +236,10 @@ def tile_picked_ycutmix_relu_po_kernel(
         weave(on_vector, z_g[0][:], z_all[0][:], 0, CHUNK)
         weave(on_vector, z_g[1][:], z_all[0][:], CHUNK, CHUNK + Z_SPLIT)
         weave(on_scalar, z_g[1][:, Z_SPLIT * PACK :], z_all[0][:], CHUNK + Z_SPLIT, HALF)
-        quant_z(0)
-        quant_z(1)
-        weave(on_vector, z_g[2][:], z_all[1][:], 0, CHUNK)
-        weave(on_vector, z_g[3][:], z_all[1][:], CHUNK, HALF)
-        quant_z(2)
-        quant_z(3)
+        quant_z(z_g[0], 0, 0, CHUNK)
+        quant_z(z_g[1], 0, CHUNK, HALF)
+        weave(on_vector, z_g[2][:], z_all[1][:], 0, HALF)
+        quant_z(z_g[2], 1, 0, HALF)
 
         layer2(0, 0, 0, CHUNK, banks[0])
         layer2(0, 0, CHUNK, HALF, banks[1])
@@ -266,10 +258,10 @@ def tile_picked_ycutmix_relu_po_kernel(
         for t in (0, 1):
             layer2(1, t, 0, HALF, banks[6 + t])
         store_y(1, 0, 2)
-        layer2(1, 2, 0, CHUNK, banks[0])
-        layer2(1, 3, 0, CHUNK, banks[1])
-        layer2(1, 2, CHUNK, HALF, banks[2])
-        layer2(1, 3, CHUNK, HALF, banks[5], on_vector)
+        for bank, first in ((banks[0], 0), (banks[1], CHUNK)):
+            for i in range(2):
+                product2(1, 2 + i, first, first + CHUNK, bank[:, i * CHUNK : (i + 1) * CHUNK])
+            on_scalar(y[1][:, 2:4, first : first + CHUNK], bank[:, 0:HALF].rearrange("p (t c) -> p t c", t=2))
         store_y(1, 2, 2)
         store_words(0)
         weave(on_vector, y_g[2][:], y[1][:], 0, CHUNK)
@@ -279,4 +271,5 @@ def tile_picked_ycutmix_relu_po_kernel(
         quant_y(3)
         store_words(1)
         for q in range(QUADRANTS):
-            nc.scalar.dma_start(out_2[0, 4 * q : 4 * q + 4, :].bitcast(I32), y_s[32 * q : 32 * q + 4, :].bitcast(I32))
+            queue = nc.sync if q < QUADRANTS // 2 else nc.scalar
+            queue.dma_start(out_2[0, 4 * q : 4 * q + 4, :].bitcast(I32), y_s[32 * q : 32 * q + 4, :].bitcast(I32))

@@ -29,7 +29,6 @@ CHUNK = 128
 SIDE = 64
 PAD = 16
 SPARE = 8
-Z_SPLIT = 64
 Y_SPLIT = 56
 FLOPS = 2 * 2 * 512 * 512 * 512
 
@@ -112,7 +111,7 @@ def tile_picked_ycutmix_relu_po_kernel(
         round_w1(on_scalar, 0, 0)
         round_w1(on_scalar, 0, 1)
         quant_w1(0)
-        pieces = ((0, HALF), (HALF, S))
+        pieces = ((0, HALF), (HALF, HALF + CHUNK), (HALF + CHUNK, S))
         for first, last in pieces:
             entries = offs_t[:, first // ENTRIES : last // ENTRIES]
             nc.vector.tensor_copy(xq_w[:, first:last], xw[:].bitcast(U32).indirect(entries))
@@ -156,10 +155,9 @@ def tile_picked_ycutmix_relu_po_kernel(
         gather(on_vector, 0)
         quant_w1(3)
         w2_g = keep.tile([P, PACK, P, PACK], BF16, name="w2_g", tag="w1_g1", align_bytes=64)
-        low_dst, low_src = w2_g[:, 0:2].rearrange("p t m s -> p m s t"), w2_cols[:, :, :, 0:2]
         nc.gpsimd.tensor_scalar(
             w2_g[:, 2:4].rearrange("p t m s -> p m t s"), w2_cols[:, :, :, 2:4].rearrange("p m s t -> p m t s"),
-            1.0, 0.0, MULT, ADD,
+            1.0, z[3][:, S : S + 1], MULT, ADD,
         )
         gather(on_scalar_indirect, 1)
         for half in range(2):
@@ -172,7 +170,7 @@ def tile_picked_ycutmix_relu_po_kernel(
         gather(on_scalar_indirect, 2)
         gather(on_scalar_indirect, 3)
         scatter(on_scalar_indirect, 2)
-        nc.vector.tensor_scalar_add(low_dst, low_src, z[3][:, S : S + 1])
+        on_vector(w2_g[:, 0:2].rearrange("p t m s -> p m s t"), w2_cols[:, :, :, 0:2])
         scatter(on_vector, 3)
         nc.vector.quantize_mx(
             out=w2_c[:].bitcast(FP8X4), scales=w2_s[:], in_=w2_g[:].rearrange("p t m s -> p (t m s)")
@@ -234,8 +232,7 @@ def tile_picked_ycutmix_relu_po_kernel(
             nc.sync.dma_start(out_words[:, cols], y_c[:, cols].bitcast(I32))
 
         weave(on_vector, z_g[0][:], z_all[0][:], 0, CHUNK)
-        weave(on_vector, z_g[1][:], z_all[0][:], CHUNK, CHUNK + Z_SPLIT)
-        weave(on_scalar, z_g[1][:, Z_SPLIT * PACK :], z_all[0][:], CHUNK + Z_SPLIT, HALF)
+        weave(on_scalar, z_g[1][:], z_all[0][:], CHUNK, HALF)
         quant_z(z_g[0], 0, 0, CHUNK)
         quant_z(z_g[1], 0, CHUNK, HALF)
         weave(on_vector, z_g[2][:], z_all[1][:], 0, HALF)

@@ -29,7 +29,10 @@ CHUNK = 128
 SIDE = 64
 PAD = 16
 SPARE = 8
+Z_SPLIT = 64
 Y_SPLIT = 56
+CLEAR_PARTS = 2
+ROUND_PARTS = 4
 FLOPS = 2 * 2 * 512 * 512 * 512
 
 
@@ -57,7 +60,9 @@ def tile_picked_ycutmix_relu_po_kernel(
             for half in range(2)
         ]
 
-        nc.vector.memset(xs[:].bitcast(I32), 0)
+        xs_words = xs[:].bitcast(I32)
+        for part in range(CLEAR_PARTS):
+            nc.vector.memset(xs_words[:, part * (T // 4) // CLEAR_PARTS : (part + 1) * (T // 4) // CLEAR_PARTS], 0)
         w1_rows = w1.rearrange("(p j) c -> p j c", j=PACK)
         nc.sync.dma_start(offs_t[:], offs)
         nc.sync.dma_start(w1_raw[0][:, 0 : PACK - 1], w1_rows[:, 0 : PACK - 1, 0:HALF])
@@ -89,13 +94,15 @@ def tile_picked_ycutmix_relu_po_kernel(
         nc.scalar.copy(z[3][:, S : S + SPARE], zeros[:])
         on_vector, on_scalar = nc.vector.tensor_copy, nc.scalar.copy
 
-        def round_w1(copy, half, pair):
+        def round_w1(copy, half, pair, parts=1):
             src = w1_raw[half][:].rearrange("p j (m s) -> p m j s", s=PACK)[:, :, :, 2 * pair : 2 * pair + 2]
             if pair == 0:
                 dst = w1_g[0][:, half].rearrange("p (s m) j -> p m j s", s=2)
             else:
                 dst = w1_g[1][:, :, SIDE * half : SIDE * (half + 1)].rearrange("p s m j -> p m j s")
-            copy(dst, src)
+            step = SIDE // parts
+            for m in range(0, SIDE, step):
+                copy(dst[:, m : m + step], src[:, m : m + step])
 
         def quant_w1(plane):
             woven = w1_g[plane // 2][:, plane % 2].rearrange("p m j -> p (m j)")
@@ -109,7 +116,7 @@ def tile_picked_ycutmix_relu_po_kernel(
             nc.scalar.activation(z[plane][:, first:last], bank[:, 0 : last - first], RELU)
 
         round_w1(on_scalar, 0, 0)
-        round_w1(on_scalar, 0, 1)
+        round_w1(on_scalar, 0, 1, ROUND_PARTS)
         quant_w1(0)
         pieces = ((0, HALF), (HALF, HALF + CHUNK), (HALF + CHUNK, S))
         for first, last in pieces:
@@ -176,15 +183,13 @@ def tile_picked_ycutmix_relu_po_kernel(
             out=w2_c[:].bitcast(FP8X4), scales=w2_s[:], in_=w2_g[:].rearrange("p t m s -> p (t m s)")
         )
         on_scalar(z_all[0][:, 2, :], z[2][:, 0:HALF])
-        on_scalar(z_all[0][:, 3, :], z[3][:, 0:HALF])
+        on_scalar(z_all[0][:, 3, 0:CHUNK], z[3][:, 0:CHUNK])
+        on_scalar(z_all[0][:, 3, CHUNK:HALF], z[3][:, CHUNK:HALF])
         on_scalar(z_all[1][:, 2, :], z[2][:, HALF:S])
         on_scalar(z_all[1][:, 3, :], z[3][:, HALF:S])
 
         chunks = S // CHUNK
-        z_g = [
-            keep.tile([P, width * PACK], BF16, name=f"z_g{c}", align_bytes=64)
-            for c, width in enumerate((CHUNK, CHUNK, HALF))
-        ]
+        z_g = [keep.tile([P, CHUNK * PACK], BF16, name=f"z_g{c}", align_bytes=64) for c in range(chunks)]
         z_c = [keep.tile([P, HALF], U32, name=f"z_c{half}", align_bytes=64) for half in range(2)]
         z_s = [keep.tile([P, HALF], U8, name=f"z_s{half}", align_bytes=64) for half in range(2)]
         y = [
@@ -205,20 +210,17 @@ def tile_picked_ycutmix_relu_po_kernel(
                 rows[:, :, first:last].rearrange("p s (a i) -> p a s i", i=2),
             )
 
-        def quant_z(woven, half, first, last):
-            cols = slice(first, last)
-            nc.vector.quantize_mx(out=z_c[half][:, cols].bitcast(FP8X4), scales=z_s[half][:, cols], in_=woven[:])
+        def quant_z(c):
+            cols = slice((c % 2) * CHUNK, (c % 2 + 1) * CHUNK)
+            nc.vector.quantize_mx(out=z_c[c // 2][:, cols].bitcast(FP8X4), scales=z_s[c // 2][:, cols], in_=z_g[c][:])
 
-        def product2(half, t, first, last, out):
+        def layer2(half, t, first, last, bank, copy=on_scalar):
             nc.tensor.matmul_mx(
-                out=out,
+                out=bank[:, 0 : last - first],
                 lhsT=w2_c[:, t * P : (t + 1) * P].bitcast(FP8X4), lhsT_scale=w2_s[:, t * P : (t + 1) * P],
                 rhs=z_c[half][:, first:last].bitcast(FP8X4), rhs_scale=z_s[half][:, first:last], start=True, stop=True,
             )
-
-        def layer2(half, t, first, last, bank):
-            product2(half, t, first, last, bank[:, 0 : last - first])
-            on_scalar(y[half][:, t, first:last], bank[:, 0 : last - first])
+            copy(y[half][:, t, first:last], bank[:, 0 : last - first])
 
         def store_y(half, t, count):
             nc.sync.dma_start(out_rows[:, t : t + count, half * HALF : (half + 1) * HALF], y[half][:, t : t + count, :])
@@ -232,11 +234,14 @@ def tile_picked_ycutmix_relu_po_kernel(
             nc.sync.dma_start(out_words[:, cols], y_c[:, cols].bitcast(I32))
 
         weave(on_vector, z_g[0][:], z_all[0][:], 0, CHUNK)
-        weave(on_scalar, z_g[1][:], z_all[0][:], CHUNK, HALF)
-        quant_z(z_g[0], 0, 0, CHUNK)
-        quant_z(z_g[1], 0, CHUNK, HALF)
-        weave(on_vector, z_g[2][:], z_all[1][:], 0, HALF)
-        quant_z(z_g[2], 1, 0, HALF)
+        weave(on_vector, z_g[1][:], z_all[0][:], CHUNK, CHUNK + Z_SPLIT)
+        weave(on_scalar, z_g[1][:, Z_SPLIT * PACK :], z_all[0][:], CHUNK + Z_SPLIT, HALF)
+        quant_z(0)
+        quant_z(1)
+        weave(on_vector, z_g[2][:], z_all[1][:], 0, CHUNK)
+        weave(on_vector, z_g[3][:], z_all[1][:], CHUNK, HALF)
+        quant_z(2)
+        quant_z(3)
 
         layer2(0, 0, 0, CHUNK, banks[0])
         layer2(0, 0, CHUNK, HALF, banks[1])
@@ -255,10 +260,10 @@ def tile_picked_ycutmix_relu_po_kernel(
         for t in (0, 1):
             layer2(1, t, 0, HALF, banks[6 + t])
         store_y(1, 0, 2)
-        for bank, first in ((banks[0], 0), (banks[1], CHUNK)):
-            for i in range(2):
-                product2(1, 2 + i, first, first + CHUNK, bank[:, i * CHUNK : (i + 1) * CHUNK])
-            on_scalar(y[1][:, 2:4, first : first + CHUNK], bank[:, 0:HALF].rearrange("p (t c) -> p t c", t=2))
+        layer2(1, 2, 0, CHUNK, banks[0])
+        layer2(1, 3, 0, CHUNK, banks[1])
+        layer2(1, 2, CHUNK, HALF, banks[2])
+        layer2(1, 3, CHUNK, HALF, banks[5], on_vector)
         store_y(1, 2, 2)
         store_words(0)
         weave(on_vector, y_g[2][:], y[1][:], 0, CHUNK)
@@ -268,5 +273,4 @@ def tile_picked_ycutmix_relu_po_kernel(
         quant_y(3)
         store_words(1)
         for q in range(QUADRANTS):
-            queue = nc.sync if q < QUADRANTS // 2 else nc.scalar
-            queue.dma_start(out_2[0, 4 * q : 4 * q + 4, :].bitcast(I32), y_s[32 * q : 32 * q + 4, :].bitcast(I32))
+            nc.scalar.dma_start(out_2[0, 4 * q : 4 * q + 4, :].bitcast(I32), y_s[32 * q : 32 * q + 4, :].bitcast(I32))

from contextlib import ExitStack

import concourse.mybir as mybir

F32 = mybir.dt.float32
BF16 = mybir.dt.bfloat16
I32 = mybir.dt.int32
U32 = mybir.dt.uint32
U16 = mybir.dt.uint16
U8 = mybir.dt.uint8
FP8X4 = mybir.dt.float8_e4m3fn_x4
RELU = mybir.ActivationFunctionType.Relu
COPY = mybir.ActivationFunctionType.Copy
ADD = mybir.AluOpType.add
MULT = mybir.AluOpType.mult

P = 128
PACK = 4
T = 1024
S = 512
H = 512
N = 512
V = 128
ENTRIES = 16
QUADRANTS = 4
BANKS = 8
HALF = 256
CHUNK = 128
SIDE = 64
PAD = 16
SPARE = 8
Z_SPLIT = 64
Y_SPLIT = 56
CLEAR_PARTS = 2
ROUND_PARTS = 4
FLOPS = 2 * 2 * 512 * 512 * 512


def tile_picked_ycutmix_relu_po_kernel(
    tc, x_words, x_scales, w1, w2, offs, give, take, out_0, out_1, out_2
):
    nc = tc.nc
    with ExitStack() as ctx:
        lists = ctx.enter_context(tc.tile_pool(name="lists", bufs=1))
        keep = ctx.enter_context(tc.tile_pool(name="keep", bufs=1))
        psum = ctx.enter_context(tc.psum_pool(name="psum", bufs=1))

        offs_t = lists.tile([P, S // ENTRIES], U16, name="offs_t")
        give_t = lists.tile([P, V // ENTRIES], U16, name="give_t")
        take_t = lists.tile([P, V // ENTRIES], U16, name="take_t")

        xw = keep.tile([P, T], I32, name="xw", align_bytes=64)
        xs = keep.tile([P, T], U8, name="xs", align_bytes=64)
        w1_raw = [
            keep.tile([P, PACK, HALF + PAD], F32, name=f"w1_raw{half}", align_bytes=256)[:, :, 0:HALF] for half in range(2)
        ]
        w2_raw = keep.tile([P, PACK, N], F32, name="w2_raw", align_bytes=64)
        z_all = [
            keep.tile([P, PACK, HALF + PAD], F32, name=f"z_all{half}", tag=f"z_all{half}", align_bytes=256)[:, :, 0:HALF]
            for half in range(2)
        ]

        xs_words = xs[:].bitcast(I32)
        for part in range(CLEAR_PARTS):
            nc.vector.memset(xs_words[:, part * (T // 4) // CLEAR_PARTS : (part + 1) * (T // 4) // CLEAR_PARTS], 0)
        w1_rows = w1.rearrange("(p j) c -> p j c", j=PACK)
        nc.sync.dma_start(offs_t[:], offs)
        nc.sync.dma_start(w1_raw[0][:, 0 : PACK - 1], w1_rows[:, 0 : PACK - 1, 0:HALF])
        for q in range(QUADRANTS):
            nc.sync.dma_start(xs[32 * q : 32 * q + 4, :].bitcast(I32), x_scales[0, 4 * q : 4 * q + 4, :].bitcast(I32))
        nc.sync.dma_start(w1_raw[0][:, PACK - 1], w1_rows[:, PACK - 1, 0:HALF])
        nc.sync.dma_start(xw[:], x_words[0].rearrange("p n t -> p (n t)").bitcast(I32))
        nc.sync.dma_start(w1_raw[1][:], w1_rows[:, :, HALF:H])
        nc.sync.dma_start(give_t[:], give)
        nc.sync.dma_start(take_t[:], take)
        nc.sync.dma_start(w2_raw[:], w2.rearrange("(p s) n -> p s n", s=PACK))

        xq_w = keep.tile([P, S], U32, name="xq_w", align_bytes=64)
        xq_s = keep.tile([P, S], U8, name="xq_s", align_bytes=64)
        nc.vector.tensor_copy(xq_s[:], xs[:].indirect(offs_t[:]))

        w1_g = [
            keep.tile([P, 2, P, PACK], BF16, name=f"w1_g{pair}", tag=f"w1_g{pair}", align_bytes=64) for pair in range(2)
        ]
        w1_c = [keep.tile([P, P], U32, name=f"w1_c{plane}", align_bytes=64) for plane in range(PACK)]
        w1_s = [keep.tile([P, P], U8, name=f"w1_s{plane}", align_bytes=64) for plane in range(PACK)]
        banks = [psum.tile([P, 512], F32, name=f"bank{b}") for b in range(BANKS)]
        z = [
            keep.tile([P, S + (SPARE if plane == 3 else 0)], F32, name=f"z{plane}", align_bytes=64)
            for plane in range(PACK)
        ]
        zeros = keep.tile([P, SPARE], F32, name="zeros", align_bytes=64)
        nc.gpsimd.memset(zeros[:], 0.0)
        nc.scalar.copy(z[3][:, S : S + SPARE], zeros[:])
        on_vector, on_scalar = nc.vector.tensor_copy, nc.scalar.copy

        def round_w1(copy, half, pair, parts=1):
            src = w1_raw[half][:].rearrange("p j (m s) -> p m j s", s=PACK)[:, :, :, 2 * pair : 2 * pair + 2]
            if pair == 0:
                dst = w1_g[0][:, half].rearrange("p (s m) j -> p m j s", s=2)
            else:
                dst = w1_g[1][:, :, SIDE * half : SIDE * (half + 1)].rearrange("p s m j -> p m j s")
            step = SIDE // parts
            for m in range(0, SIDE, step):
                copy(dst[:, m : m + step], src[:, m : m + step])

        def quant_w1(plane):
            woven = w1_g[plane // 2][:, plane % 2].rearrange("p m j -> p (m j)")
            nc.vector.quantize_mx(out=w1_c[plane][:].bitcast(FP8X4), scales=w1_s[plane][:], in_=woven)

        def layer1(plane, first, last, bank):
            nc.tensor.matmul_mx(
                out=bank[:, 0 : last - first], lhsT=w1_c[plane][:].bitcast(FP8X4), lhsT_scale=w1_s[plane][:],
                rhs=xq_w[:, first:last].bitcast(FP8X4), rhs_scale=xq_s[:, first:last], start=True, stop=True,
            )
            nc.scalar.activation(z[plane][:, first:last], bank[:, 0 : last - first], RELU)

        round_w1(on_scalar, 0, 0)
        round_w1(on_scalar, 0, 1, ROUND_PARTS)
        quant_w1(0)
        pieces = ((0, HALF), (HALF, HALF + CHUNK), (HALF + CHUNK, S))
        for first, last in pieces:
            entries = offs_t[:, first // ENTRIES : last // ENTRIES]
            nc.vector.tensor_copy(xq_w[:, first:last], xw[:].bitcast(U32).indirect(entries))
        round_w1(on_vector, 1, 0)
        round_w1(on_vector, 1, 1)
        quant_w1(1)
        quant_w1(2)
        for b, (first, last) in enumerate(pieces):
            layer1(0, first, last, banks[b])
        for half in range(2):
            layer1(1, half * HALF, (half + 1) * HALF, banks[3 + half])

        picked = [
            keep.tile(
                [P, V], F32, name=f"picked{plane}", tag="w1_g0" if plane == 0 else f"picked{plane}", align_bytes=64
            )
            for plane in range(PACK)
        ]

        def on_scalar_indirect(dst, src):
            nc.scalar.activation(dst, src, COPY)

        def gather(copy, plane):
            copy(picked[plane][:], z[plane][:].indirect(give_t[:]))

        def scatter(copy, plane):
            copy(z[plane][:].indirect(take_t[:]), picked[plane][:])

        def move(plane):
            for half in range(2):
                for s in range(2):
                    nc.sync.dma_start(
                        z_all[half][SIDE * plane : SIDE * (plane + 1), s, :],
                        z[plane][SIDE * s : SIDE * (s + 1), half * HALF : (half + 1) * HALF],
                    )

        w2_c = keep.tile([P, N], U32, name="w2_c", align_bytes=64)
        w2_s = keep.tile([P, N], U8, name="w2_s", align_bytes=64)
        w2_cols = w2_raw[:].rearrange("p s (m t) -> p m s t", t=PACK)

        gather(on_vector, 0)
        quant_w1(3)
        w2_g = keep.tile([P, PACK, P, PACK], BF16, name="w2_g", tag="w1_g1", align_bytes=64)
        nc.gpsimd.tensor_scalar(
            w2_g[:, 2:4].rearrange("p t m s -> p m t s"), w2_cols[:, :, :, 2:4].rearrange("p m s t -> p m t s"),
            1.0, z[3][:, S : S + 1], MULT, ADD,
        )
        gather(on_scalar_indirect, 1)
        for half in range(2):
            layer1(2, half * HALF, (half + 1) * HALF, banks[5 + half])
        scatter(on_vector, 0)
        move(0)
        scatter(on_vector, 1)
        move(1)
        layer1(3, 0, S, banks[7])
        gather(on_scalar_indirect, 2)
        gather(on_scalar_indirect, 3)
        scatter(on_scalar_indirect, 2)
        on_vector(w2_g[:, 0:2].rearrange("p t m s -> p m s t"), w2_cols[:, :, :, 0:2])
        scatter(on_vector, 3)
        nc.vector.quantize_mx(
            out=w2_c[:].bitcast(FP8X4), scales=w2_s[:], in_=w2_g[:].rearrange("p t m s -> p (t m s)")
        )
        on_scalar(z_all[0][:, 2, :], z[2][:, 0:HALF])
        on_scalar(z_all[0][:, 3, 0:CHUNK], z[3][:, 0:CHUNK])
        on_scalar(z_all[0][:, 3, CHUNK:HALF], z[3][:, CHUNK:HALF])
        on_scalar(z_all[1][:, 2, :], z[2][:, HALF:S])
        on_scalar(z_all[1][:, 3, :], z[3][:, HALF:S])

        chunks = S // CHUNK
        z_g = [keep.tile([P, CHUNK * PACK], BF16, name=f"z_g{c}", align_bytes=64) for c in range(chunks)]
        z_c = [keep.tile([P, HALF], U32, name=f"z_c{half}", align_bytes=64) for half in range(2)]
        z_s = [keep.tile([P, HALF], U8, name=f"z_s{half}", align_bytes=64) for half in range(2)]
        y = [
            keep.tile([P, PACK, HALF + PAD], F32, name=f"y{half}", tag=("y0", "y1")[half], align_bytes=256)[
                :, :, 0:HALF
            ]
            for half in range(2)
        ]
        y_g = [keep.tile([P, CHUNK * PACK], BF16, name=f"y_g{c}", align_bytes=64) for c in range(chunks)]
        y_c = keep.tile([P, S], U32, name="y_c", align_bytes=64)
        y_s = keep.tile([P, S], U8, name="y_s", align_bytes=64)
        out_rows = out_0.rearrange("(p t) c -> p t c", t=PACK)
        out_words = out_1[0].rearrange("p n t -> p (n t)").bitcast(I32)

        def weave(copy, woven, rows, first, last):
            copy(
                woven[:, 0 : (last - first) * PACK].rearrange("p (a i s) -> p a s i", i=2, s=PACK),
                rows[:, :, first:last].rearrange("p s (a i) -> p a s i", i=2),
            )

        def quant_z(c):
            cols = slice((c % 2) * CHUNK, (c % 2 + 1) * CHUNK)
            nc.vector.quantize_mx(out=z_c[c // 2][:, cols].bitcast(FP8X4), scales=z_s[c // 2][:, cols], in_=z_g[c][:])

        def layer2(half, t, first, last, bank, copy=on_scalar):
            nc.tensor.matmul_mx(
                out=bank[:, 0 : last - first],
                lhsT=w2_c[:, t * P : (t + 1) * P].bitcast(FP8X4), lhsT_scale=w2_s[:, t * P : (t + 1) * P],
                rhs=z_c[half][:, first:last].bitcast(FP8X4), rhs_scale=z_s[half][:, first:last], start=True, stop=True,
            )
            copy(y[half][:, t, first:last], bank[:, 0 : last - first])

        def store_y(half, t, count):
            nc.sync.dma_start(out_rows[:, t : t + count, half * HALF : (half + 1) * HALF], y[half][:, t : t + count, :])

        def quant_y(c):
            cols = slice(c * CHUNK, (c + 1) * CHUNK)
            nc.vector.quantize_mx(out=y_c[:, cols].bitcast(FP8X4), scales=y_s[:, cols], in_=y_g[c][:])

        def store_words(half):
            cols = slice(half * HALF, (half + 1) * HALF)
            nc.sync.dma_start(out_words[:, cols], y_c[:, cols].bitcast(I32))

        weave(on_vector, z_g[0][:], z_all[0][:], 0, CHUNK)
        weave(on_vector, z_g[1][:], z_all[0][:], CHUNK, CHUNK + Z_SPLIT)
        weave(on_scalar, z_g[1][:, Z_SPLIT * PACK :], z_all[0][:], CHUNK + Z_SPLIT, HALF)
        quant_z(0)
        quant_z(1)
        weave(on_vector, z_g[2][:], z_all[1][:], 0, CHUNK)
        weave(on_vector, z_g[3][:], z_all[1][:], CHUNK, HALF)
        quant_z(2)
        quant_z(3)

        layer2(0, 0, 0, CHUNK, banks[0])
        layer2(0, 0, CHUNK, HALF, banks[1])
        store_y(0, 0, 1)
        for t in (1, 2):
            layer2(0, t, 0, HALF, banks[1 + t])
            store_y(0, t, 1)
        layer2(0, 3, 0, CHUNK, banks[4])
        layer2(0, 3, CHUNK, HALF, banks[5])
        store_y(0, 3, 1)
        weave(on_vector, y_g[0][:], y[0][:], 0, CHUNK)
        weave(on_vector, y_g[1][:], y[0][:], CHUNK, HALF)
        quant_y(0)
        quant_y(1)

        for t in (0, 1):
            layer2(1, t, 0, HALF, banks[6 + t])
        store_y(1, 0, 2)
        layer2(1, 2, 0, CHUNK, banks[0])
        layer2(1, 3, 0, CHUNK, banks[1])
        layer2(1, 2, CHUNK, HALF, banks[2])
        layer2(1, 3, CHUNK, HALF, banks[5], on_vector)
        store_y(1, 2, 2)
        store_words(0)
        weave(on_vector, y_g[2][:], y[1][:], 0, CHUNK)
        weave(on_vector, y_g[3][:], y[1][:], CHUNK, CHUNK + Y_SPLIT)
        weave(on_scalar, y_g[3][:, Y_SPLIT * PACK :], y[1][:], CHUNK + Y_SPLIT, HALF)
        quant_y(2)
        quant_y(3)
        store_words(1)
        for q in range(QUADRANTS):
            nc.scalar.dma_start(out_2[0, 4 * q : 4 * q + 4, :].bitcast(I32), y_s[32 * q : 32 * q + 4, :].bitcast(I32))
